import numpy as np, ml_dtypes
CORES = [24,25,26,27,28,29,30,31]
N = 8
BF = ml_dtypes.bfloat16
def gentries(a):
    return np.ascontiguousarray(a.reshape(8, 16, -1).transpose(0, 2, 1)).reshape(8, -1)
def gtable(e):
    e = np.asarray(e); return np.ascontiguousarray(e.reshape(8, -1, 16).transpose(0, 2, 1)).reshape(128, -1).astype(np.int32)
D, UG, B, A, NB, KG = 4, 8, 6, 2, 32, 16
U, V, E, S, K = 8 * UG, 2 ** B, 2 ** (A * B), 16 * NB, 8 * KG // N
def stored(c):
    return np.ascontiguousarray(c.reshape(N, 8, UG, NB, 16).transpose(0, 1, 4, 3, 2)).reshape(N, 128, -1).astype(np.int32)
def unstored(x):
    return np.ascontiguousarray(x.reshape(N, 8, 16, NB, UG).transpose(0, 1, 4, 3, 2)).reshape(N, U, S).astype(np.int64)
def pack(t, c, gv, wr):
    return {"tb": t.reshape(N, 8, -1).astype(np.float32).astype(BF), "x": stored(c), "give": np.stack([gtable(v.reshape(8, -1)) for v in gv]), "wires": np.stack([gtable(v.reshape(8, -1)) for v in wr])}
def draw(rng):
    return rng.integers(0, V, (N, 8, D, UG, E)), rng.integers(0, V, (N, U, S)), rng.integers(0, U, (N, 8, D, KG)), rng.integers(0, N * K, (N, 8, D, A, UG))
def setup_inputs(rng):
    return pack(*draw(rng))
def setup_inputs_ends(rng):
    t, c, gv, wr = draw(rng)
    t = rng.integers(0, 2, t.shape) * (V - 1); t[..., 0] = 0; t[..., E - 1] = V - 1; c = rng.integers(0, 2, c.shape) * (V - 1); c[:, :, 0] = 0; c[:, :, S - 1] = V - 1
    gv = rng.choice(np.array([0, UG - 1, UG, 7 * UG, U - 1]), gv.shape); wr = rng.choice(np.array([0, K - 1, K, N * K - K, N * K - 1]), wr.shape)
    return pack(t, c, gv, wr)
def setup_inputs_one(rng):
    t, c, gv, wr = draw(rng)
    gv[:] = gv[..., :1].copy(); wr[:] = wr[:, :, :, :1].copy(); q = rng.integers(0, N); wr[q] = wr[q][..., :1].copy()
    return pack(t, c, gv, wr)
def setup_inputs_next(rng):
    t, c, gv, wr = draw(rng)
    i = rng.integers(0, 2, (N, 8, D, UG, 1)) * (A - 1); t = (np.arange(E) >> (B * (A - 1 - i))) & (V - 1)
    wr = wr % K + K * ((np.arange(N) + 1) % N).reshape(N, 1, 1, 1, 1)
    return pack(t, c, gv, wr)
def setup_inputs_spread(rng):
    t, c, gv, wr = draw(rng)
    t = t >> rng.integers(0, B + 1, (N, 8, D, UG, 1)); c = c >> rng.integers(0, B + 1, (N, U, 1))
    gv = (rng.random(gv.shape) ** 3 * U).astype(np.int64); wr = (rng.random(wr.shape) ** 3 * (N * K)).astype(np.int64)
    return pack(t, c, gv, wr)
def check_inputs(d):
    bad = []
    for name, top in (("x", V), ("give", U), ("wires", N * K)):
        if not ((d[name] >= 0) & (d[name] < top)).all(): bad.append(name)
    t = d["tb"].astype(np.float32)
    if not ((t >= 0) & (t < V) & (np.floor(t) == t)).all(): bad.append("tb")
    return bad
def reference(tb, x, give, wires):
    t = tb.astype(np.float32).astype(np.int64).reshape(N, 8, D, UG, E)
    gv = np.stack([gentries(v) for v in give]).reshape(N, 8 * D * KG).reshape(N, 8, D, KG)
    wr = np.stack([gentries(v) for v in wires]).reshape(N, 8, D, A, UG)
    c = unstored(x)
    for l in range(D):
        lines = np.zeros((N, N * K, S), np.int64); new = np.zeros((N, U, S), np.int64)
        for q in range(N):
            lines[:, q * K:(q + 1) * K] = c[q][gv[q, :, l].reshape(-1)].reshape(N, K, S)
        for r in range(N):
            a = np.zeros((8, UG, S), np.int64)
            for i in range(A):
                a = a * V + lines[r][wr[r, :, l, i]]
            new[r] = np.take_along_axis(t[r, :, l], a, axis=2).reshape(U, S)
        c = new
    return {"y": np.asarray(stored(c), np.float32)}

@@ -1,0 +1,463 @@
+from concourse.bass import DstId, RemoteDMATransfer
+from concourse.mybir import dt, AluOpType, AxisListType, ActivationFunctionType
+
+BF, F32, I32, U16 = "bfloat16", "float32", "int32", "uint16"
+D = 4
+
+SCRATCH = {}
+for _t, _names in ((BF, "xb0 128 xb1 128 xt0 128 xt1 128 diag 512 oh 512 glb 32 gmk 32 cmpb 4 sel0 128 sel1 128 sel2 128 sel3 128 "
+                        "rr0 2048 rr1 2048 tab0 4096 tab1 4096 tab3 8192 rowq 128 rowe 128 rowa 128 row16 16 rowu 64 rows 128 "
+                        "rowm 32 mask 32 rho3 128 rho4 128 zrow 144 ones 128 amat 128 bmq 64 bmn 64 base 576 pmat 768 e0 128 "
+                        "ev 64 od 64 selb 128"),
+                   (F32, "wf 4 wqf 4 ysb0 256 ysb1 256 pcol 1 k4f 4 pf 8 hf 1 u2f 1"),
+                   (I32, "xi0 128 xi1 128 gl 32 wi 4 wqi 4 pint 1 k4i 4 k4j 4 pk 8"),
+                   (U16, "offs0 128 offs1 128 lst 64")):
+    _w = _names.split()
+    for _k in range(0, len(_w), 2):
+        SCRATCH[_w[_k]] = ("sbuf", [128, int(_w[_k + 1])], _t)
+for _e in range(4):
+    for _b in range(2):
+        SCRATCH["land%d%d" % (_e, _b)] = ("sbuf", [128, 1024], BF)
+for _n in ("psg0", "psg1", "psg2", "psg3", "psa0", "psa1", "psm", "psw"):
+    SCRATCH[_n] = ("psum", [128, 512], F32)
+
+SEMAPHORES = ["qv", "qs", "qp", "qg", "loc", "dgive", "dwire", "dx0", "dx1", "dt0", "dt1", "dt3", "dy", "arrg"]
+SEMAPHORES += ["arr%d%d" % (_e, _b) for _e in range(4) for _b in range(2)]
+
+
+def rank_program(g, core, T, topo):
+    rank = T.rank_of(core)
+    if rank is None:
+        return
+    cores = T.cores
+    N = len(cores)
+    Op = AluOpType
+    Copy = ActivationFunctionType.Copy
+    queues = {"v": g.vector, "s": g.scalar, "p": g.tensor, "g": g, "y": g.sync}
+    count = {}
+    seen = {}
+
+    def need(q, *tokens):
+        want = {}
+        for name, val in tokens:
+            want[name] = max(val, want.get(name, 0))
+        for name in sorted(want):
+            if seen.get((q, name), 0) < want[name]:
+                queues[q].wait_ge(T.sem[name], want[name])
+                seen[(q, name)] = want[name]
+
+    def done(q, inst):
+        name = "q" + q
+        count[name] = count.get(name, 0) + 1
+        inst.then_inc(T.sem[name], 1)
+        return (name, count[name])
+
+    def dma(q, out, in_, name):
+        count[name] = count.get(name, 0) + 16
+        queues[q].dma_start(out, in_).then_inc(T.sem[name], 16)
+        return (name, count[name])
+
+    def ts(out, in0, s1, s2, op0, op1=None):
+        if op1 is None:
+            return done("v", g.vector.tensor_scalar(out, in0, s1, s2, op0))
+        return done("v", g.vector.tensor_scalar(out, in0, s1, s2, op0, op1))
+
+    def copy(q, out, in_):
+        if q == "v":
+            return done("v", g.vector.tensor_copy(out, in_))
+        return done("s", g.scalar.activation(out, in_, Copy))
+
+    def iota(out, pattern, base, mult, whole=False):
+        if whole:
+            return done("g", g.iota(out, pattern, base, mult))
+        return done("g", g.iota(out, pattern, base, mult, allow_small_or_imprecise_dtypes=True))
+
+    def mm(out, lhsT, rhs, start, stop):
+        return g.tensor.matmul(out, lhsT, rhs, start, stop)
+
+    others = [cores[(rank + k) % N] for k in range(1, N)]
+    engines = topo.mask(core, others[0])
+    for dst in others:
+        engines &= topo.mask(core, dst)
+    n_eng = len([k for k in topo.engines(core, others[0]) if engines >> k & 1])
+    arrive = n_eng * len(others)
+
+    def send(name, arr, lo, hi, *tokens):
+        need("g", *tokens)
+        ids = [DstId(rid=topo.addr(dst)[0], pnc=topo.addr(dst)[1]) for dst in others]
+        part = T[name][:, lo:hi]
+        g.remote_dma_fused([RemoteDMATransfer(dst_ids=ids, dma_engine_mask=engines, remote_sem=T.sem[arr],
+                                              srcs=[part], dsts=[part] * len(others))], local_sem=T.sem["loc"])
+        count["loc"] = count.get("loc", 0) + n_eng
+
+    t_x = {}
+
+    def load_x(q, b, gb):
+        for z in range(2):
+            at = 128 * b + 64 * z
+            t_x[b] = dma(q, T["xi%d" % b][z::2, 64 * gb:64 * gb + 64], T.x[64 * gb:64 * gb + 64, at:at + 64], "dx%d" % b)
+
+    t_give = dma("y", T.gl[:, 4 * rank:4 * rank + 4], T.give[:, :], "dgive")
+    load_x("s", 0, 0)
+    load_x("y", 0, 1)
+    load_x("s", 1, 0)
+    load_x("y", 1, 1)
+    t_wire = dma("y", T.wi[:], T.wires[:, :], "dwire")
+    W = 8 * 4096
+    t_tab = {}
+    dma("y", T.tab0[0::2, :], T.tb[:, 0:W], "dt0")
+    t_tab[0] = t_tab[1] = dma("y", T.tab0[1::2, :], T.tb[:, W:2 * W], "dt0")
+
+    i_pcol = iota(T.pcol[:], [[0, 1]], 0, 1)
+    i_pint = iota(T.pint[:], [[0, 1]], 0, 1, True)
+    i_rowe = iota(T.rowe[:], [[8, 4], [32, 4], [1, 8]], 0, 0)
+    i_rowq = iota(T.rowq[:], [[1, 128]], 0, 0)
+    i_rows = iota(T.rows[:], [[0, 8], [1, 16]], 16 * rank, 0)
+    i_rowm = iota(T.rowm[:], [[1, 8], [0, 4]], 0, 0)
+    i_row16 = iota(T.row16[:], [[1, 2], [2, 8]], 0, 0)
+    send("gl", "arrg", 4 * rank, 4 * rank + 4, t_give)
+
+    pc = T.pcol[:, 0:1]
+    zero = [done("v", g.vector.memset(T.tab3[:, 0:512], 0.0)), done("v", g.vector.memset(T.tab3[:, 512:1536], 0.0))]
+
+    def clear(q, a, b):
+        part = T.tab3[:, a:b]
+        if q == "g":
+            zero.append(iota(part, [[0, b - a]], 0, 0))
+        else:
+            need("s", zero[0])
+            zero.append(copy("s", part, T.tab3[:, 0:b - a]))
+
+    for k in range(3, 6):
+        clear("s", 512 * k, 512 * k + 512)
+    c_ones = done("v", g.vector.memset(T.ones[:], 1.0))
+    need("v", i_pint, i_rowe)
+    c_e0 = ts(T.e0[:], T.rowe[:], pc, None, Op.is_equal)
+
+    def bits(k, shift, mask):
+        if shift:
+            return ts(T.pk[:, k:k + 1], T.pint[:], shift, mask, Op.arith_shift_right, Op.bitwise_and)
+        return ts(T.pk[:, k:k + 1], T.pint[:], mask, None, Op.bitwise_and)
+
+    for k, (sh, mk) in enumerate(((0, 7), (3, 15), (4, 7), (0, 8), (0, 4), (0, 112))):
+        c_i = bits(k, sh, mk)
+    p7, p3, pq, h8, u4, g16 = [T.pf[:, k:k + 1] for k in range(6)]
+    need("v", i_rowq)
+    perms = {}
+    perms[0] = perms[1] = ts(T.pmat[:, 128:256], T.rowq[:], pc, None, Op.is_equal)
+    need("v", c_i)
+    c_f = copy("v", T.pf[:, 0:6], T.pk[:, 0:6])
+
+    def codes(b):
+        need("v", t_x[b])
+        x1 = copy("v", T["xb%d" % b][:], T["xi%d" % b][:])
+        need("v", x1)
+        x2 = done("v", g.vector.transpose(T["xt%d" % b][:], T["xb%d" % b][:]))
+        need("p", x2, c_e0)
+        toks = []
+        for gb in range(2):
+            for z in range(2):
+                inst = mm(T["psg%d" % (2 * b + gb)][64 * z:64 * z + 64, 0:64], T["xt%d" % b][:, 64 * gb:64 * gb + 64],
+                          T.e0[:, 64 * z:64 * z + 64], True, True)
+            toks.append(done("p", inst))
+        return toks
+
+    t_own = {}
+
+    def first(q, b, gb, tok):
+        need(q, tok)
+        for c in range(2):
+            at = 128 * rank + 64 * c + 32 * gb
+            t = copy(q, T["land0%d" % b][:, at:at + 32], T["psg%d" % (2 * b + gb)][:, 32 * c:32 * c + 32])
+        t_own.setdefault((0, b), []).append(t)
+
+    def evac(q, e, b, c, tok):
+        need(q, tok)
+        at = 128 * rank + 64 * c
+        t = copy(q, T["land%d%d" % (e, b)][:, at:at + 64], T["psg%d" % (2 * b + c)][:, 0:64])
+        t_own.setdefault((e, b), []).append(t)
+
+    def send_codes(e, b):
+        send("land%d%d" % (e, b), "arr%d%d" % (e, b), 128 * rank, 128 * rank + 128, *t_own[(e, b)])
+
+    def diag(e):
+        return done("s", g.scalar.activation(T.diag[:, 128 * e:128 * e + 128], T.pmat[:, 128:256], Copy, scale=T.wf[:, e:e + 1]))
+
+    p_x0 = codes(0)
+    p_x1 = codes(1)
+    need("v", t_wire)
+    c_wf = copy("v", T.wf[:], T.wi[:])
+    first("s", 0, 0, p_x0[0])
+    first("v", 0, 1, p_x0[1])
+    send_codes(0, 0)
+    need("s", c_wf, perms[0])
+    c_d0 = diag(0)
+    need("p", c_ones, c_d0)
+    p_w0 = done("p", mm(T.psa0[:, 0:128], T.ones[:], T.diag[:, 0:128], True, True))
+    first("s", 1, 0, p_x1[0])
+    first("v", 1, 1, p_x1[1])
+    send_codes(0, 1)
+    for e in range(1, D):
+        c_d = diag(e)
+    need("p", c_d)
+    p_w = done("p", mm(T.psm[:, 128:512], T.ones[:], T.diag[:, 128:512], True, True))
+    i_rowa = iota(T.rowa[:], [[0, 16], [1, 8]], 0, 0)
+    i_rowu = iota(T.rowu[:], [[2, 8], [16, 8]], 0, 0)
+    i_rho3 = iota(T.rho3[:], [[2, 2], [4, 32], [1, 2]], 0, 0)
+    i_rho4 = iota(T.rho4[:], [[4, 32], [1, 2], [2, 2]], 0, 0)
+    i_k4 = iota(T.k4i[:], [[-4, 4]], 0, 1, True)
+    i_z = iota(T.zrow[:], [[16, 9], [-1000, 8], [0, 2]], 7000, 0)
+    clear("g", 6656, 8192)
+
+    x1 = ts(T.wqi[:], T.wi[:], 112, None, Op.bitwise_and)
+    need("v", i_rows)
+    c_sel = ts(T.selb[:], T.rows[:], pc, None, Op.is_equal)
+    need("v", p_w0)
+    c_oh0 = ts(T.oh[:, 0:128], T.psa0[:, 0:128], pc, None, Op.is_equal)
+    need("v", x1, c_f, i_row16)
+    c_wq = ts(T.wqf[:], T.wqi[:], 8.0, None, Op.mult)
+    c_mk = ts(T.mask[:], T.rowm[:], pq, None, Op.is_equal)
+    ts(T.hf[:], h8, 8.0, None, Op.mult)
+    need("v", c_wq)
+
+    def ranks(a, b):
+        for e in range(a, b):
+            t = ts(T.bmq[:, 16 * e:16 * e + 16], T.row16[:], p3, T.wqf[:, e:e + 1], Op.is_equal, Op.mult)
+        return t
+
+    c_bq = {0: ranks(0, 1)}
+    need("v", t_give, ("arrg", arrive))
+    c_gl = copy("v", T.glb[:], T.gl[:])
+    need("p", c_sel, c_gl)
+    p_c = done("p", mm(T.psw[:, 64:96], T.selb[:], T.glb[:], True, True))
+    need("v", i_rowa)
+    c_am = ts(T.amat[:], T.rowa[:], p7, None, Op.is_equal)
+    need("v", p_c, c_mk)
+    c_mg = done("v", g.vector.tensor_tensor(T.gmk[:], T.psw[:, 64:96], T.mask[:], Op.mult))
+    need("v", c_mg)
+
+    def units_of(e):
+        return done("v", g.vector.tensor_reduce(T.cmpb[:, e:e + 1], T.gmk[:, e:32:4], AxisListType.X, Op.max))
+
+    c_c = units_of(0)
+    need("p", c_c, c_oh0)
+    p_n = {0: done("p", mm(T.psa0[:, 128:129], T.oh[:, 0:128], T.cmpb[:, 0:1], True, True))}
+    t_l = {}
+    c_bn = {}
+    c_un = {1: units_of(1)}
+
+    def spread(e):
+        need("v", p_n[e])
+        src = T.psm[:, e:e + 1] if e else T.psa0[:, 128:129]
+        c_bn[e] = ts(T.bmn[:, 16 * e:16 * e + 16], T.row16[:], p3, src, Op.is_equal, Op.mult)
+
+    def lists(a, b):
+        need("p", c_am, c_bq[b - 1], c_bn[b - 1])
+        mm(T.psw[:, 16 * a:16 * b], T.amat[:], T.bmq[:, 16 * a:16 * b], True, False)
+        return done("p", mm(T.psw[:, 16 * a:16 * b], T.amat[:], T.bmn[:, 16 * a:16 * b], False, True))
+
+    def put_lists(a, b, tok):
+        need("v", tok)
+        t = ts(T.lst[:, 16 * a:16 * b], T.psw[:, 16 * a:16 * b], T.hf[:, 0:1], None, Op.add)
+        for e in range(a, b):
+            t_l[e] = t
+
+    spread(0)
+    perms["l0"] = lists(0, 1)
+    perms[0] = perms[1] = ts(T.pmat[:, 0:128], T.rowq[:], pc, 64.0, Op.is_equal, Op.mult)
+    c_un[2] = units_of(2)
+    put_lists(0, 1, perms["l0"])
+    for k in range(6, 9):
+        clear("s", 512 * k, 512 * k + 512)
+
+    units = {}
+    y_banks = [[T.psm, T.psw, T.psg0, T.psg1], [T.psg2, T.psg3, T.psa0, T.psa1]]
+    fin = {0: [], 1: []}
+    t_y = {}
+
+    def hot(a, b):
+        need("v", p_w)
+        t = ts(T.oh[:, 128 * a:128 * b], T.psm[:, 128 * a:128 * b], pc, None, Op.is_equal)
+        for j in range(a, b):
+            need("p", t, c_un[j])
+            inst = mm(T.psm[:, j:j + 1], T.oh[:, 128 * j:128 * j + 128], T.cmpb[:, j:j + 1], True, True)
+        t = done("p", inst)
+        for j in range(a, b):
+            p_n[j] = t
+
+    def spare(e):
+        if e == 0:
+            hot(1, 2)
+            need("v", i_rowu)
+            units[1] = units[3] = (T.ev, ts(T.ev[:], T.rowu[:], pc, None, Op.is_equal))
+        elif e == 1:
+            spread(2)
+            spread(3)
+            perms["l2"] = lists(2, D)
+            units[2] = (T.od, ts(T.od[:], T.rowu[:], 1.0, pc, Op.add, Op.is_equal))
+        elif e == 2:
+            need("v", i_rho4)
+            ts(T.pmat[:, 512:640], T.rho4[:], pc, 64.0, Op.is_equal, Op.mult)
+            perms[3] = ts(T.pmat[:, 640:768], T.rho4[:], pc, None, Op.is_equal)
+            perms["u2"] = ts(T.u2f[:], u4, 1024.0, None, Op.mult)
+
+    def between(e):
+        if e == 0:
+            put_lists(1, 2, perms["l1"])
+            c_un[3] = units_of(3)
+            hot(2, D)
+            c_bq[D - 1] = ranks(2, D)
+            clear("g", 5632, 6656)
+        elif e == 1:
+            put_lists(2, D, perms["l2"])
+            need("v", i_rho3, i_k4)
+            ts(T.pmat[:, 256:384], T.rho3[:], pc, 64.0, Op.is_equal, Op.mult)
+            perms[2] = ts(T.pmat[:, 384:512], T.rho3[:], pc, None, Op.is_equal)
+            perms["k4"] = ts(T.k4j[:], T.k4i[:], 13, None, Op.bitwise_and)
+            clear("g", 4608, 5632)
+        elif e == 2:
+            need("v", i_z, perms["k4"])
+            c1 = ts(T.k4f[:], T.k4j[:], -1000.0, g16, Op.mult, Op.add)
+            need("v", c1)
+            for v in range(4):
+                perms["base"] = ts(T.base[:, 144 * v:144 * v + 144], T.zrow[:], T.k4f[:, v:v + 1], None, Op.is_equal)
+
+    for e in range(D):
+        last = e == D - 1
+        tab = T["tab%d" % (0, 0, 1, 3)[e]]
+        pk = (0, 0, 256, 512)[e]
+        sel, pa, off = {}, {}, {}
+        tok = {}
+        pieces = {0: [(0, 30, 64), (64, 80, 96), (96, 112, 128)],
+                  1: [(0, 16, 32), (32, 48, 64), (64, 80, 96), (96, 112, 128)] if last else [(0, 16, 32), (32, 48, 64), (64, 96, 128)]}
+
+        def pick(q, b):
+            i = 0 if q == "v" else 1
+            need(q, ("arr%d%d" % (e, b), arrive), t_l[e], *t_own[(e, b)])
+            sel[(q, b)] = copy(q, T["sel%d" % (2 * b + i)][:], T["land%d%d" % (e, b)][:, 0:1024].indirect(T.lst[:, 16 * e + 8 * i:16 * e + 8 * i + 8]))
+
+        def halves(b):
+            return [(T.psa0, 0, 64), (T.psg2, 64, 128)] if b == 0 else [(T.psa1, 0, 128)]
+
+        def turn(b):
+            need("p", perms[e], *t_own[(e, 1)])
+            pa[b] = []
+            for bank, lo, hi in halves(b):
+                for i, q in enumerate("vs"):
+                    need("p", sel[(q, b)])
+                    at = pk + 128 * i
+                    inst = mm(bank[:, lo:hi], T["sel%d" % (2 * b + i)][:], T.pmat[:, at + lo:at + hi], i == 0, i == 1)
+                pa[b].append(done("p", inst))
+
+        def cast(b):
+            off[b] = []
+            for t, (bank, lo, hi) in zip(pa[b], halves(b)):
+                need("v", t)
+                o, i = T["offs%d" % b][:, lo:hi], bank[:, lo:hi]
+                off[b].append(ts(o, i, T.u2f[:, 0:1], None, Op.add) if last else copy("v", o, i))
+
+        def look(q, b, j):
+            x, y, z = pieces[b][j]
+            lo, hi = (x, y) if q == "v" else (y, z)
+            need(q, t_tab[e], off[b][0 if j == 0 else -1])
+            win = tab[:, 0:8192 if last else 4096].indirect(T["offs%d" % b][:, lo:hi])
+            tok[(q, b, j)] = copy(q, T["rr%d" % b][:, 16 * lo:16 * hi], win)
+
+        def give(b, c):
+            hit = [k for k in range(len(pieces[b])) if pieces[b][k][2] == 64 * c + 64][0]
+            mat, c_mat = units[e + 1]
+            need("p", tok[("v", b, hit)], tok[("s", b, hit)], c_mat)
+            for u in range(8):
+                inst = mm(T["psg%d" % (2 * b + c)][:, u:64:8], T["rr%d" % b][:, 1024 * c + u:1024 * c + 1024:8],
+                          mat[:, 8 * u:8 * u + 8], True, True)
+            return done("p", inst)
+
+        p_y = {}
+
+        def place(b, j):
+            x, y, z = pieces[b][j]
+            blocks = [(k, v) for k in range(x // 16, z // 16) for v in range(4)]
+            if z == 128:
+                blocks = [(k, v) for v in range(4) for k in range(x // 16, z // 16)]
+            for k, v in blocks:
+                if 16 * k < y:
+                    need("p", tok[("v", b, j)])
+                if 16 * k + 16 > y:
+                    need("p", tok[("s", b, j)])
+                at = 144 * v + 14 - 2 * k
+                inst = mm(y_banks[b][v][:, 0:64], T.base[:, at:at + 128], T["rr%d" % b][:, 256 * k + v:256 * k + 256:4], k == 0, k == 7)
+                if k == 7:
+                    p_y[(b, v)] = done("p", inst)
+
+        def out(q, b, v):
+            need(q, p_y[(b, v)])
+            fin[b].append(copy(q, T["ysb%d" % b][:, v:256:4], y_banks[b][v][:, 0:64]))
+
+        def store(b, queue):
+            for k in range(2):
+                need(queue[k], *fin[b])
+                t_y[k] = dma(queue[k], T.y[k::2, 128 * b:128 * b + 128], T["ysb%d" % b][k::2, 128 * k:128 * k + 128], "dy")
+
+        for q in "vs":
+            pick(q, 0)
+        turn(0)
+        spare(e)
+        if last:
+            need("v", perms["u2"])
+            need("p", perms["base"])
+        cast(0)
+        for k in range(3):
+            if k == 2:
+                for q in "vs":
+                    pick(q, 1)
+            for q in "vs":
+                look(q, 0, k)
+        if last:
+            place(0, 0)
+            turn(1)
+            place(0, 1)
+            place(0, 2)
+            cast(1)
+        else:
+            p0 = [give(0, 0)]
+            turn(1)
+            p0.append(give(0, 1))
+            cast(1)
+            evac("v", e + 1, 0, 0, p0[0])
+            if e == 0:
+                c_bq[1] = ranks(1, 2)
+                spread(1)
+                perms["l1"] = lists(1, 2)
+        for k in range(len(pieces[1])):
+            for q in "vs":
+                look(q, 1, k)
+            if k == 0 and not last:
+                evac("s", e + 1, 0, 1, p0[1])
+                send_codes(e + 1, 0)
+            if k == 1 and last:
+                for v, q in enumerate("vsvs"):
+                    out(q, 0, v)
+                store(0, "yy")
+        need("y", ("arr%d1" % e, arrive))
+        if e == 0:
+            dma("y", T.tab1[0::2, :], T.tb[:, 2 * W:3 * W], "dt1")
+        elif e == 1:
+            t_tab[2] = dma("y", T.tab1[1::2, :], T.tb[:, 2 * W:3 * W], "dt1")
+        elif e == 2:
+            need("y", *zero)
+            dma("y", T.tab3[0::4, 0:4096], T.tb[:, 3 * W:3 * W + W // 2], "dt3")
+            t_tab[3] = dma("y", T.tab3[2::4, 4096:8192], T.tb[:, 3 * W + W // 2:4 * W], "dt3")
+        if last:
+            for k in range(len(pieces[1])):
+                place(1, k)
+            for v, q in enumerate("vsvs"):
+                out(q, 1, v)
+            store(1, "ys")
+            need("y", *t_y.values())
+            break
+        p1 = [give(1, c) for c in range(2)]
+        evac("v", e + 1, 1, 0, p1[0])
+        evac("s", e + 1, 1, 1, p1[1])
+        send_codes(e + 1, 1)
+        between(e)
+    need("g", *[(n, count[n]) for n in ("qv", "qs", "qp", "qg", "loc")])

@@ -1,28 +1,32 @@
 from concourse.bass import DstId, RemoteDMATransfer
 from concourse.mybir import dt, AluOpType, AxisListType, ActivationFunctionType
 
-BF, F32, I32, U16 = "bfloat16", "float32", "int32", "uint16"
+BF, F32, I32, U16, F16 = "bfloat16", "float32", "int32", "uint16", "float16"
 D = 4
+STEPS = 4 * D
+RW = 64
+SEL = 264
 
 SCRATCH = {}
-for _t, _names in ((BF, "xb0 128 xb1 128 xt0 128 xt1 128 diag 512 oh 512 glb 32 gmk 32 cmpb 4 sel0 128 sel1 128 sel2 128 sel3 128 "
-                        "rr0 2048 rr1 2048 tab0 4096 tab1 4096 tab3 8192 rowq 128 rowe 128 rowa 128 row16 16 rowu 64 rows 128 "
-                        "rowm 32 mask 32 rho3 128 rho4 128 zrow 144 ones 128 amat 128 bmq 64 bmn 64 base 576 pmat 768 e0 128 "
-                        "ev 64 od 64 selb 128"),
-                   (F32, "wf 4 wqf 4 ysb0 256 ysb1 256 pcol 1 k4f 4 pf 8 hf 1 u2f 1"),
-                   (I32, "xi0 128 xi1 128 gl 32 wi 4 wqi 4 pint 1 k4i 4 k4j 4 pk 8"),
-                   (U16, "offs0 128 offs1 128 lst 64")):
+for _t, _names in ((BF, "xb0 128 xb1 128 xt0 128 xt1 128 oht 512 oh 512 glb 32 sel 528 rr0 1024 rr1 1024 tab0 4096 tab1 4096 "
+                        "rowq 128 rowe 128 rowa 128 rho 128 rowd 8 pmat 512 e0 128 land0 2560 land1 2560 land2 2560 land3 2560"),
+                   (F16, "amat 128 bm 32"),
+                   (F32, "wkf 4 wqf 4 ysb0 128 ysb1 128 pcol 1 pf 2 step 32 col 32"),
+                   (I32, "xi0 128 xi1 128 gl 32 wi 4 wki 4 wqi 4 pint 1 pk 2"),
+                   (U16, "offs0 64 offs1 64 lst 32")):
     _w = _names.split()
     for _k in range(0, len(_w), 2):
         SCRATCH[_w[_k]] = ("sbuf", [128, int(_w[_k + 1])], _t)
-for _e in range(4):
-    for _b in range(2):
-        SCRATCH["land%d%d" % (_e, _b)] = ("sbuf", [128, 1024], BF)
 for _n in ("psg0", "psg1", "psg2", "psg3", "psa0", "psa1", "psm", "psw"):
     SCRATCH[_n] = ("psum", [128, 512], F32)
 
-SEMAPHORES = ["qv", "qs", "qp", "qg", "loc", "dgive", "dwire", "dx0", "dx1", "dt0", "dt1", "dt3", "dy", "arrg"]
-SEMAPHORES += ["arr%d%d" % (_e, _b) for _e in range(4) for _b in range(2)]
+SEMAPHORES = ["qv", "qs", "qp", "qg", "loc", "dgive", "dwire", "dx0", "dx1", "dt0", "dt1", "dy", "arrg"]
+SEMAPHORES += ["arr%d" % _n for _n in range(STEPS)]
+
+CUT = (26, 30, 38)
+CUT_LAST = {15: (32, 64, 64)}
+HALF, EARLY, EVAC = 0, 0, "v"
+LOADS = {0: [0], 1: [1, 2], 2: [3], 3: [4], 4: [5], 5: [6], 6: [7]}
 
 
 def rank_program(g, core, T, topo):
@@ -67,9 +71,7 @@ def rank_program(g, core, T, topo):
             return done("v", g.vector.tensor_copy(out, in_))
         return done("s", g.scalar.activation(out, in_, Copy))
 
-    def iota(out, pattern, base, mult, whole=False):
-        if whole:
-            return done("g", g.iota(out, pattern, base, mult))
+    def iota(out, pattern, base, mult):
         return done("g", g.iota(out, pattern, base, mult, allow_small_or_imprecise_dtypes=True))
 
     def mm(out, lhsT, rhs, start, stop):
@@ -97,56 +99,45 @@ def rank_program(g, core, T, topo):
             at = 128 * b + 64 * z
             t_x[b] = dma(q, T["xi%d" % b][z::2, 64 * gb:64 * gb + 64], T.x[64 * gb:64 * gb + 64, at:at + 64], "dx%d" % b)
 
-    t_give = dma("y", T.gl[:, 4 * rank:4 * rank + 4], T.give[:, :], "dgive")
+    mine = 4 * (N - 1 - rank)
+    t_give = dma("y", T.gl[:, mine:mine + 4], T.give[:, :], "dgive")
     load_x("s", 0, 0)
     load_x("y", 0, 1)
     load_x("s", 1, 0)
     load_x("y", 1, 1)
-    t_wire = dma("y", T.wi[:], T.wires[:, :], "dwire")
+    t_wire = dma("s", T.wi[:], T.wires[:, :], "dwire")
     W = 8 * 4096
     t_tab = {}
     dma("y", T.tab0[0::2, :], T.tb[:, 0:W], "dt0")
     t_tab[0] = t_tab[1] = dma("y", T.tab0[1::2, :], T.tb[:, W:2 * W], "dt0")
 
+    def load_tables(k):
+        e, j = 2 + k // 4, k % 4
+        t_tab[2] = t_tab[3] = dma("y", T.tab1[32 * j + e % 2:32 * j + 32:2, :], T.tb[2 * j:2 * j + 2, e * W:e * W + W], "dt1")
+
     i_pcol = iota(T.pcol[:], [[0, 1]], 0, 1)
-    i_pint = iota(T.pint[:], [[0, 1]], 0, 1, True)
     i_rowe = iota(T.rowe[:], [[8, 4], [32, 4], [1, 8]], 0, 0)
     i_rowq = iota(T.rowq[:], [[1, 128]], 0, 0)
-    i_rows = iota(T.rows[:], [[0, 8], [1, 16]], 16 * rank, 0)
-    i_rowm = iota(T.rowm[:], [[1, 8], [0, 4]], 0, 0)
-    i_row16 = iota(T.row16[:], [[1, 2], [2, 8]], 0, 0)
-    send("gl", "arrg", 4 * rank, 4 * rank + 4, t_give)
+    send("gl", "arrg", mine, mine + 4, t_give)
 
     pc = T.pcol[:, 0:1]
-    zero = [done("v", g.vector.memset(T.tab3[:, 0:512], 0.0)), done("v", g.vector.memset(T.tab3[:, 512:1536], 0.0))]
-
-    def clear(q, a, b):
-        part = T.tab3[:, a:b]
-        if q == "g":
-            zero.append(iota(part, [[0, b - a]], 0, 0))
-        else:
-            need("s", zero[0])
-            zero.append(copy("s", part, T.tab3[:, 0:b - a]))
-
-    for k in range(3, 6):
-        clear("s", 512 * k, 512 * k + 512)
-    c_ones = done("v", g.vector.memset(T.ones[:], 1.0))
-    need("v", i_pint, i_rowe)
+    ident = T.pmat[:, 128:256]
+    c_zero = done("v", g.vector.memset(T.sel[:], 0.0))
+    need("v", i_pcol)
+    c = copy("v", T.pint[:], T.pcol[:])
+    need("v", c, i_rowe)
+    ts(T.pk[:, 0:1], T.pint[:], 104, None, Op.bitwise_and)
+    c = ts(T.pk[:, 1:2], T.pint[:], 23, None, Op.bitwise_and)
     c_e0 = ts(T.e0[:], T.rowe[:], pc, None, Op.is_equal)
+    need("v", c, i_rowq)
+    c_pf = copy("v", T.pf[:], T.pk[:])
+    c_id = ts(ident, T.rowq[:], pc, None, Op.is_equal)
+    c_rowd = ts(T.rowd[:], T.rowq[:, 0:8], 1024.0, None, Op.mult)
+    need("s", c_id)
+    perms = {0: done("s", g.scalar.activation(T.pmat[:, 0:128], ident, Copy, scale=64.0))}
 
-    def bits(k, shift, mask):
-        if shift:
-            return ts(T.pk[:, k:k + 1], T.pint[:], shift, mask, Op.arith_shift_right, Op.bitwise_and)
-        return ts(T.pk[:, k:k + 1], T.pint[:], mask, None, Op.bitwise_and)
-
-    for k, (sh, mk) in enumerate(((0, 7), (3, 15), (4, 7), (0, 8), (0, 4), (0, 112))):
-        c_i = bits(k, sh, mk)
-    p7, p3, pq, h8, u4, g16 = [T.pf[:, k:k + 1] for k in range(6)]
-    need("v", i_rowq)
-    perms = {}
-    perms[0] = perms[1] = ts(T.pmat[:, 128:256], T.rowq[:], pc, None, Op.is_equal)
-    need("v", c_i)
-    c_f = copy("v", T.pf[:, 0:6], T.pk[:, 0:6])
+    t_own = {}
+    p_x = {}
 
     def codes(b):
         need("v", t_x[b])
@@ -154,310 +145,173 @@ def rank_program(g, core, T, topo):
         need("v", x1)
         x2 = done("v", g.vector.transpose(T["xt%d" % b][:], T["xb%d" % b][:]))
         need("p", x2, c_e0)
-        toks = []
-        for gb in range(2):
-            for z in range(2):
-                inst = mm(T["psg%d" % (2 * b + gb)][64 * z:64 * z + 64, 0:64], T["xt%d" % b][:, 64 * gb:64 * gb + 64],
-                          T.e0[:, 64 * z:64 * z + 64], True, True)
-            toks.append(done("p", inst))
-        return toks
+        for b0 in range(2):
+            for gb in range(2):
+                for z in range(2):
+                    at = 64 * z + 32 * b0
+                    inst = mm(T["psg%d" % (2 * b + b0)][64 * z:64 * z + 64, 32 * gb:32 * gb + 32],
+                              T["xt%d" % b][:, 64 * gb:64 * gb + 64], T.e0[:, at:at + 32], True, True)
+            p_x[2 * b + b0] = done("p", inst)
 
-    t_own = {}
-
-    def first(q, b, gb, tok):
+    def hand_on(n, tok, q="s"):
         need(q, tok)
-        for c in range(2):
-            at = 128 * rank + 64 * c + 32 * gb
-            t = copy(q, T["land0%d" % b][:, at:at + 32], T["psg%d" % (2 * b + gb)][:, 32 * c:32 * c + 32])
-        t_own.setdefault((0, b), []).append(t)
+        at = 8 * RW * (n % 4) + RW * rank
+        t_own[n] = copy(q, T["land%d" % (n // 4)][:, at:at + RW], T["psg%d" % (n % 4)][:, 0:RW])
+        send("land%d" % (n // 4), "arr%d" % n, at, at + RW, t_own[n])
 
-    def evac(q, e, b, c, tok):
-        need(q, tok)
-        at = 128 * rank + 64 * c
-        t = copy(q, T["land%d%d" % (e, b)][:, at:at + 64], T["psg%d" % (2 * b + c)][:, 0:64])
-        t_own.setdefault((e, b), []).append(t)
+    codes(0)
+    codes(1)
+    hand_on(0, p_x[0])
+    i_rowa = iota(T.rowa[:], [[0, 8], [16, 2], [1, 8]], 0, 0)
+    hand_on(1, p_x[1])
+    i_rho = iota(T.rho[:], [[1, 32], [32, 2], [64, 2]], 0, 0)
+    hand_on(2, p_x[2])
+    hand_on(3, p_x[3])
 
-    def send_codes(e, b):
-        send("land%d%d" % (e, b), "arr%d%d" % (e, b), 128 * rank, 128 * rank + 128, *t_own[(e, b)])
-
-    def diag(e):
-        return done("s", g.scalar.activation(T.diag[:, 128 * e:128 * e + 128], T.pmat[:, 128:256], Copy, scale=T.wf[:, e:e + 1]))
-
-    p_x0 = codes(0)
-    p_x1 = codes(1)
     need("v", t_wire)
-    c_wf = copy("v", T.wf[:], T.wi[:])
-    first("s", 0, 0, p_x0[0])
-    first("v", 0, 1, p_x0[1])
-    send_codes(0, 0)
-    need("s", c_wf, perms[0])
-    c_d0 = diag(0)
-    need("p", c_ones, c_d0)
-    p_w0 = done("p", mm(T.psa0[:, 0:128], T.ones[:], T.diag[:, 0:128], True, True))
-    first("s", 1, 0, p_x1[0])
-    first("v", 1, 1, p_x1[1])
-    send_codes(0, 1)
-    for e in range(1, D):
-        c_d = diag(e)
-    need("p", c_d)
-    p_w = done("p", mm(T.psm[:, 128:512], T.ones[:], T.diag[:, 128:512], True, True))
-    i_rowa = iota(T.rowa[:], [[0, 16], [1, 8]], 0, 0)
-    i_rowu = iota(T.rowu[:], [[2, 8], [16, 8]], 0, 0)
-    i_rho3 = iota(T.rho3[:], [[2, 2], [4, 32], [1, 2]], 0, 0)
-    i_rho4 = iota(T.rho4[:], [[4, 32], [1, 2], [2, 2]], 0, 0)
-    i_k4 = iota(T.k4i[:], [[-4, 4]], 0, 1, True)
-    i_z = iota(T.zrow[:], [[16, 9], [-1000, 8], [0, 2]], 7000, 0)
-    clear("g", 6656, 8192)
+    ts(T.wki[:], T.wi[:], 15, None, Op.bitwise_and)
+    c = ts(T.wqi[:], T.wi[:], 112, None, Op.bitwise_and)
+    need("v", c)
+    ts(T.wkf[:], T.wki[:], 16.0 * rank, None, Op.add)
+    c = ts(T.wqf[:], T.wqi[:], 64.0, -8192.0 + RW, Op.mult, Op.add)
+    need("v", c, c_rowd)
+    c_oh = {}
+    c_step = {}
 
-    x1 = ts(T.wqi[:], T.wi[:], 112, None, Op.bitwise_and)
-    need("v", i_rows)
-    c_sel = ts(T.selb[:], T.rows[:], pc, None, Op.is_equal)
-    need("v", p_w0)
-    c_oh0 = ts(T.oh[:, 0:128], T.psa0[:, 0:128], pc, None, Op.is_equal)
-    need("v", x1, c_f, i_row16)
-    c_wq = ts(T.wqf[:], T.wqi[:], 8.0, None, Op.mult)
-    c_mk = ts(T.mask[:], T.rowm[:], pq, None, Op.is_equal)
-    ts(T.hf[:], h8, 8.0, None, Op.mult)
-    need("v", c_wq)
-
-    def ranks(a, b):
+    def hot(a, b, bank):
         for e in range(a, b):
-            t = ts(T.bmq[:, 16 * e:16 * e + 16], T.row16[:], p3, T.wqf[:, e:e + 1], Op.is_equal, Op.mult)
-        return t
+            t = ts(T.oht[:, 128 * e:128 * e + 128], T.rowq[:], T.wkf[:, e:e + 1], None, Op.is_equal)
+            need("p", t, c_id)
+            inst = mm(bank[:, 128 * e:128 * e + 128], T.oht[:, 128 * e:128 * e + 128], ident, True, True)
+        need("s", done("p", inst))
+        c_oh[a] = copy("s", T.oh[:, 128 * a:128 * b], bank[:, 128 * a:128 * b])
+        for e in range(a, b):
+            c_step[a] = ts(T.step[:, 8 * e:8 * e + 8], T.rowd[:], T.wqf[:, e:e + 1], float(RW), Op.add, Op.min)
 
-    c_bq = {0: ranks(0, 1)}
+    hot(0, 1, T.psa0)
+    need("v", i_rowa, c_pf)
+    c_am = ts(T.amat[:], T.rowa[:], T.pf[:, 1:2], None, Op.is_equal)
+    hot(1, D, T.psm)
+    need("v", i_rho)
+    c_rho = ts(T.pmat[:, 384:512], T.rho[:], pc, None, Op.is_equal)
+    need("s", c_rho)
+    perms[D - 1] = done("s", g.scalar.activation(T.pmat[:, 256:384], T.pmat[:, 384:512], Copy, scale=64.0))
+
     need("v", t_give, ("arrg", arrive))
     c_gl = copy("v", T.glb[:], T.gl[:])
-    need("p", c_sel, c_gl)
-    p_c = done("p", mm(T.psw[:, 64:96], T.selb[:], T.glb[:], True, True))
-    need("v", i_rowa)
-    c_am = ts(T.amat[:], T.rowa[:], p7, None, Op.is_equal)
-    need("v", p_c, c_mk)
-    c_mg = done("v", g.vector.tensor_tensor(T.gmk[:], T.psw[:, 64:96], T.mask[:], Op.mult))
-    need("v", c_mg)
-
-    def units_of(e):
-        return done("v", g.vector.tensor_reduce(T.cmpb[:, e:e + 1], T.gmk[:, e:32:4], AxisListType.X, Op.max))
-
-    c_c = units_of(0)
-    need("p", c_c, c_oh0)
-    p_n = {0: done("p", mm(T.psa0[:, 128:129], T.oh[:, 0:128], T.cmpb[:, 0:1], True, True))}
     t_l = {}
-    c_bn = {}
-    c_un = {1: units_of(1)}
+    hold = {}
 
-    def spread(e):
-        need("v", p_n[e])
-        src = T.psm[:, e:e + 1] if e else T.psa0[:, 128:129]
-        c_bn[e] = ts(T.bmn[:, 16 * e:16 * e + 16], T.row16[:], p3, src, Op.is_equal, Op.mult)
+    def units(a, b, bank):
+        need("p", c_gl, c_oh[a])
+        for e in range(a, b):
+            inst = mm(bank[:, 8 * e:8 * e + 8], T.oh[:, 128 * e:128 * e + 128], T.glb[:, e:32:4], True, True)
+        hold["u", a] = done("p", inst)
 
-    def lists(a, b):
-        need("p", c_am, c_bq[b - 1], c_bn[b - 1])
-        mm(T.psw[:, 16 * a:16 * b], T.amat[:], T.bmq[:, 16 * a:16 * b], True, False)
-        return done("p", mm(T.psw[:, 16 * a:16 * b], T.amat[:], T.bmn[:, 16 * a:16 * b], False, True))
+    def columns(a, b, bank):
+        need("v", hold["u", a], c_step[a])
+        hold["c", a] = done("v", g.vector.tensor_tensor_scan(T.col[:, 8 * a:8 * b], T.step[:, 8 * a:8 * b], bank[:, 8 * a:8 * b],
+                                                             0.0, Op.add, Op.max))
 
-    def put_lists(a, b, tok):
-        need("v", tok)
-        t = ts(T.lst[:, 16 * a:16 * b], T.psw[:, 16 * a:16 * b], T.hf[:, 0:1], None, Op.add)
+    def spread(a, b, bank):
+        need("v", hold["c", a])
+        for e in range(a, b):
+            t = ts(T.bm[:, 8 * e:8 * e + 8], T.rowe[:, 0:64:8], T.pf[:, 0:1], T.col[:, 8 * e + 7:8 * e + 8], Op.is_equal, Op.mult)
+        need("p", t, c_am)
+        hold["l", a] = done("p", mm(bank[:, 64 + 8 * a:64 + 8 * b], T.amat[:], T.bm[:, 8 * a:8 * b], True, True))
+
+    def put(a, b, bank):
+        need("v", hold["l", a])
+        t = copy("v", T.lst[:, 8 * a:8 * b], bank[:, 64 + 8 * a:64 + 8 * b])
         for e in range(a, b):
             t_l[e] = t
 
-    spread(0)
-    perms["l0"] = lists(0, 1)
-    perms[0] = perms[1] = ts(T.pmat[:, 0:128], T.rowq[:], pc, 64.0, Op.is_equal, Op.mult)
-    c_un[2] = units_of(2)
-    put_lists(0, 1, perms["l0"])
-    for k in range(6, 9):
-        clear("s", 512 * k, 512 * k + 512)
+    units(0, 1, T.psw)
+    units(1, D, T.psm)
+    columns(0, 1, T.psw)
+    spread(0, 1, T.psw)
+    columns(1, D, T.psm)
+    put(0, 1, T.psw)
 
-    units = {}
-    y_banks = [[T.psm, T.psw, T.psg0, T.psg1], [T.psg2, T.psg3, T.psa0, T.psa1]]
-    fin = {0: [], 1: []}
-    t_y = {}
+    off, tok = {}, {}
 
-    def hot(a, b):
-        need("v", p_w)
-        t = ts(T.oh[:, 128 * a:128 * b], T.psm[:, 128 * a:128 * b], pc, None, Op.is_equal)
-        for j in range(a, b):
-            need("p", t, c_un[j])
-            inst = mm(T.psm[:, j:j + 1], T.oh[:, 128 * j:128 * j + 128], T.cmpb[:, j:j + 1], True, True)
-        t = done("p", inst)
-        for j in range(a, b):
-            p_n[j] = t
+    def pick(n):
+        e, at = n // 4, SEL * (n % 2)
+        need("s", ("arr%d" % n, arrive), t_l[e], t_own[n], c_zero)
+        win = T["land%d" % e][:, 8 * RW * (n % 4):8 * RW * (n % 4 + 1)]
+        return copy("s", T.sel[:, at + 1:at + 257:2], win.indirect(T.lst[:, 8 * e:8 * e + 8]))
 
-    def spare(e):
-        if e == 0:
-            hot(1, 2)
-            need("v", i_rowu)
-            units[1] = units[3] = (T.ev, ts(T.ev[:], T.rowu[:], pc, None, Op.is_equal))
-        elif e == 1:
-            spread(2)
-            spread(3)
-            perms["l2"] = lists(2, D)
-            units[2] = (T.od, ts(T.od[:], T.rowu[:], 1.0, pc, Op.add, Op.is_equal))
-        elif e == 2:
-            need("v", i_rho4)
-            ts(T.pmat[:, 512:640], T.rho4[:], pc, 64.0, Op.is_equal, Op.mult)
-            perms[3] = ts(T.pmat[:, 640:768], T.rho4[:], pc, None, Op.is_equal)
-            perms["u2"] = ts(T.u2f[:], u4, 1024.0, None, Op.mult)
+    def turn(n, t):
+        e, at = n // 4, SEL * (n % 2)
+        pk = 256 if e == D - 1 else 0
+        need("p", t, perms[D - 1 if e == D - 1 else 0])
+        for i in range(2):
+            for z in range(2):
+                a, b = at + 128 * i + 1 - z, pk + 128 * i + 64 * z
+                inst = mm(T["psa%d" % (n % 2)][:, 0:64], T.sel[:, a:a + 128], T.pmat[:, b:b + 64], i + z == 0, i + z == 2)
+        hold["a", n] = done("p", inst)
 
-    def between(e):
-        if e == 0:
-            put_lists(1, 2, perms["l1"])
-            c_un[3] = units_of(3)
-            hot(2, D)
-            c_bq[D - 1] = ranks(2, D)
-            clear("g", 5632, 6656)
-        elif e == 1:
-            put_lists(2, D, perms["l2"])
-            need("v", i_rho3, i_k4)
-            ts(T.pmat[:, 256:384], T.rho3[:], pc, 64.0, Op.is_equal, Op.mult)
-            perms[2] = ts(T.pmat[:, 384:512], T.rho3[:], pc, None, Op.is_equal)
-            perms["k4"] = ts(T.k4j[:], T.k4i[:], 13, None, Op.bitwise_and)
-            clear("g", 4608, 5632)
-        elif e == 2:
-            need("v", i_z, perms["k4"])
-            c1 = ts(T.k4f[:], T.k4j[:], -1000.0, g16, Op.mult, Op.add)
-            need("v", c1)
-            for v in range(4):
-                perms["base"] = ts(T.base[:, 144 * v:144 * v + 144], T.zrow[:], T.k4f[:, v:v + 1], None, Op.is_equal)
+    def cast(n):
+        need("v", hold["a", n])
+        off[n] = copy("v", T["offs%d" % (n % 2)][:], T["psa%d" % (n % 2)][:, 0:64])
 
-    for e in range(D):
-        last = e == D - 1
-        tab = T["tab%d" % (0, 0, 1, 3)[e]]
-        pk = (0, 0, 256, 512)[e]
-        sel, pa, off = {}, {}, {}
-        tok = {}
-        pieces = {0: [(0, 30, 64), (64, 80, 96), (96, 112, 128)],
-                  1: [(0, 16, 32), (32, 48, 64), (64, 80, 96), (96, 112, 128)] if last else [(0, 16, 32), (32, 48, 64), (64, 96, 128)]}
+    def look(q, n, lo, hi):
+        if lo < hi:
+            need(q, t_tab[n // 4], off[n])
+            win = T["tab%d" % (n // 8)][:, :].indirect(T["offs%d" % (n % 2)][:, lo:hi])
+            tok[q, n] = copy(q, T["rr%d" % (n % 2)][:, 16 * lo:16 * hi], win)
 
-        def pick(q, b):
-            i = 0 if q == "v" else 1
-            need(q, ("arr%d%d" % (e, b), arrive), t_l[e], *t_own[(e, b)])
-            sel[(q, b)] = copy(q, T["sel%d" % (2 * b + i)][:], T["land%d%d" % (e, b)][:, 0:1024].indirect(T.lst[:, 16 * e + 8 * i:16 * e + 8 * i + 8]))
-
-        def halves(b):
-            return [(T.psa0, 0, 64), (T.psg2, 64, 128)] if b == 0 else [(T.psa1, 0, 128)]
-
-        def turn(b):
-            need("p", perms[e], *t_own[(e, 1)])
-            pa[b] = []
-            for bank, lo, hi in halves(b):
-                for i, q in enumerate("vs"):
-                    need("p", sel[(q, b)])
-                    at = pk + 128 * i
-                    inst = mm(bank[:, lo:hi], T["sel%d" % (2 * b + i)][:], T.pmat[:, at + lo:at + hi], i == 0, i == 1)
-                pa[b].append(done("p", inst))
-
-        def cast(b):
-            off[b] = []
-            for t, (bank, lo, hi) in zip(pa[b], halves(b)):
-                need("v", t)
-                o, i = T["offs%d" % b][:, lo:hi], bank[:, lo:hi]
-                off[b].append(ts(o, i, T.u2f[:, 0:1], None, Op.add) if last else copy("v", o, i))
-
-        def look(q, b, j):
-            x, y, z = pieces[b][j]
-            lo, hi = (x, y) if q == "v" else (y, z)
-            need(q, t_tab[e], off[b][0 if j == 0 else -1])
-            win = tab[:, 0:8192 if last else 4096].indirect(T["offs%d" % b][:, lo:hi])
-            tok[(q, b, j)] = copy(q, T["rr%d" % b][:, 16 * lo:16 * hi], win)
-
-        def give(b, c):
-            hit = [k for k in range(len(pieces[b])) if pieces[b][k][2] == 64 * c + 64][0]
-            mat, c_mat = units[e + 1]
-            need("p", tok[("v", b, hit)], tok[("s", b, hit)], c_mat)
+    def take(n, lo, hi):
+        e = n // 4
+        need("p", tok["v", n], tok["s", n])
+        for z in range(2):
             for u in range(8):
-                inst = mm(T["psg%d" % (2 * b + c)][:, u:64:8], T["rr%d" % b][:, 1024 * c + u:1024 * c + 1024:8],
-                          mat[:, 8 * u:8 * u + 8], True, True)
-            return done("p", inst)
+                if e < D - 1:
+                    out = T["psg%d" % (n % 4)][64 * z + lo:64 * z + hi, u:64:8]
+                else:
+                    out = T["psg%d" % (n % 4 // 2)][64 * z + lo:64 * z + hi, 8 * (n % 2) + u:128:16]
+                inst = mm(out, T["rr%d" % (n % 2)][:, 16 * lo + 2 * u + z:16 * hi:16], T.pmat[:, 128 + 2 * u + e % 2:256:16], True, True)
+        return done("p", inst)
 
-        p_y = {}
+    def store(b, tok_p, q, queue):
+        need(q, tok_p)
+        t = copy(q, T["ysb%d" % b][:], T["psg%d" % b][:, 0:128])
+        for k in range(8):
+            need(queue[k % 2], t)
+            hold["y"] = dma(queue[k % 2], T.y[16 * k:16 * k + 16, 128 * b:128 * b + 128], T["ysb%d" % b][:, 16 * k:16 * k + 16], "dy")
 
-        def place(b, j):
-            x, y, z = pieces[b][j]
-            blocks = [(k, v) for k in range(x // 16, z // 16) for v in range(4)]
-            if z == 128:
-                blocks = [(k, v) for v in range(4) for k in range(x // 16, z // 16)]
-            for k, v in blocks:
-                if 16 * k < y:
-                    need("p", tok[("v", b, j)])
-                if 16 * k + 16 > y:
-                    need("p", tok[("s", b, j)])
-                at = 144 * v + 14 - 2 * k
-                inst = mm(y_banks[b][v][:, 0:64], T.base[:, at:at + 128], T["rr%d" % b][:, 256 * k + v:256 * k + 256:4], k == 0, k == 7)
-                if k == 7:
-                    p_y[(b, v)] = done("p", inst)
-
-        def out(q, b, v):
-            need(q, p_y[(b, v)])
-            fin[b].append(copy(q, T["ysb%d" % b][:, v:256:4], y_banks[b][v][:, 0:64]))
-
-        def store(b, queue):
-            for k in range(2):
-                need(queue[k], *fin[b])
-                t_y[k] = dma(queue[k], T.y[k::2, 128 * b:128 * b + 128], T["ysb%d" % b][k::2, 128 * k:128 * k + 128], "dy")
-
-        for q in "vs":
-            pick(q, 0)
-        turn(0)
-        spare(e)
-        if last:
-            need("v", perms["u2"])
-            need("p", perms["base"])
-        cast(0)
-        for k in range(3):
-            if k == 2:
-                for q in "vs":
-                    pick(q, 1)
-            for q in "vs":
-                look(q, 0, k)
-        if last:
-            place(0, 0)
-            turn(1)
-            place(0, 1)
-            place(0, 2)
-            cast(1)
-        else:
-            p0 = [give(0, 0)]
-            turn(1)
-            p0.append(give(0, 1))
-            cast(1)
-            evac("v", e + 1, 0, 0, p0[0])
-            if e == 0:
-                c_bq[1] = ranks(1, 2)
-                spread(1)
-                perms["l1"] = lists(1, 2)
-        for k in range(len(pieces[1])):
-            for q in "vs":
-                look(q, 1, k)
-            if k == 0 and not last:
-                evac("s", e + 1, 0, 1, p0[1])
-                send_codes(e + 1, 0)
-            if k == 1 and last:
-                for v, q in enumerate("vsvs"):
-                    out(q, 0, v)
-                store(0, "yy")
-        need("y", ("arr%d1" % e, arrive))
-        if e == 0:
-            dma("y", T.tab1[0::2, :], T.tb[:, 2 * W:3 * W], "dt1")
-        elif e == 1:
-            t_tab[2] = dma("y", T.tab1[1::2, :], T.tb[:, 2 * W:3 * W], "dt1")
-        elif e == 2:
-            need("y", *zero)
-            dma("y", T.tab3[0::4, 0:4096], T.tb[:, 3 * W:3 * W + W // 2], "dt3")
-            t_tab[3] = dma("y", T.tab3[2::4, 4096:8192], T.tb[:, 3 * W + W // 2:4 * W], "dt3")
-        if last:
-            for k in range(len(pieces[1])):
-                place(1, k)
-            for v, q in enumerate("vsvs"):
-                out(q, 1, v)
-            store(1, "ys")
-            need("y", *t_y.values())
-            break
-        p1 = [give(1, c) for c in range(2)]
-        evac("v", e + 1, 1, 0, p1[0])
-        evac("s", e + 1, 1, 1, p1[1])
-        send_codes(e + 1, 1)
-        between(e)
+    turn(0, pick(0))
+    spread(1, D, T.psm)
+    cast(0)
+    for n in range(STEPS):
+        a, h, b = CUT_LAST.get(n, CUT)
+        more = n + 1 < STEPS
+        if n:
+            t = take(n - 1, hold["h"], 64)
+        hold["h"] = 32 if HALF else 0
+        if more and EARLY:
+            turn(n + 1, pick(n + 1))
+        look("v", n, 0, a)
+        look("s", n, a, h)
+        if n == 0:
+            put(1, D, T.psm)
+        if n and n + 3 < STEPS:
+            hand_on(n + 3, t, EVAC)
+        elif n == STEPS - 2:
+            store(0, t, EVAC, "yy")
+        if HALF:
+            take(n, 0, 32)
+        if more and not EARLY:
+            turn(n + 1, pick(n + 1))
+        if more and EARLY == 1:
+            cast(n + 1)
+        look("s", n, b, 64)
+        look("v", n, h, b)
+        if more and EARLY != 1:
+            cast(n + 1)
+        for k in LOADS.get(n, ()):
+            need("y", off[n])
+            load_tables(k)
+    store(1, take(STEPS - 1, hold["h"], 64), "v", "ys")
+    need("y", hold["y"])
     need("g", *[(n, count[n]) for n in ("qv", "qs", "qp", "qg", "loc")])

@@ -23,9 +23,9 @@ for _n in ("psg0", "psg1", "psg2", "psg3", "psa0", "psa1", "psm", "psw"):
 SEMAPHORES = ["qv", "qs", "qp", "qg", "loc", "dgive", "dwire", "dx0", "dx1", "dt0", "dt1", "dy", "arrg"]
 SEMAPHORES += ["arr%d" % _n for _n in range(STEPS)]
 
-CUT = (26, 30, 38)
-CUT_LAST = {15: (32, 64, 64)}
-HALF, EARLY, EVAC = 0, 0, "v"
+CUT = (22, 32, 44)
+CUT_LAST = {15: (16, 32, 48)}
+HALF, EARLY, EVAC = 1, 1, "v"
 LOADS = {0: [0], 1: [1, 2], 2: [3], 3: [4], 4: [5], 5: [6], 6: [7]}
 
 
@@ -118,6 +118,7 @@ def rank_program(g, core, T, topo):
     i_pcol = iota(T.pcol[:], [[0, 1]], 0, 1)
     i_rowe = iota(T.rowe[:], [[8, 4], [32, 4], [1, 8]], 0, 0)
     i_rowq = iota(T.rowq[:], [[1, 128]], 0, 0)
+    i_rowa = iota(T.rowa[:], [[0, 8], [16, 2], [1, 8]], 0, 0)
     send("gl", "arrg", mine, mine + 4, t_give)
 
     pc = T.pcol[:, 0:1]
@@ -162,11 +163,10 @@ def rank_program(g, core, T, topo):
     codes(0)
     codes(1)
     hand_on(0, p_x[0])
-    i_rowa = iota(T.rowa[:], [[0, 8], [16, 2], [1, 8]], 0, 0)
     hand_on(1, p_x[1])
-    i_rho = iota(T.rho[:], [[1, 32], [32, 2], [64, 2]], 0, 0)
     hand_on(2, p_x[2])
     hand_on(3, p_x[3])
+    i_rho = iota(T.rho[:], [[1, 32], [32, 2], [64, 2]], 0, 0)
 
     need("v", t_wire)
     ts(T.wki[:], T.wi[:], 15, None, Op.bitwise_and)
@@ -192,10 +192,6 @@ def rank_program(g, core, T, topo):
     need("v", i_rowa, c_pf)
     c_am = ts(T.amat[:], T.rowa[:], T.pf[:, 1:2], None, Op.is_equal)
     hot(1, D, T.psm)
-    need("v", i_rho)
-    c_rho = ts(T.pmat[:, 384:512], T.rho[:], pc, None, Op.is_equal)
-    need("s", c_rho)
-    perms[D - 1] = done("s", g.scalar.activation(T.pmat[:, 256:384], T.pmat[:, 384:512], Copy, scale=64.0))
 
     need("v", t_give, ("arrg", arrive))
     c_gl = copy("v", T.glb[:], T.gl[:])
@@ -282,6 +278,9 @@ def rank_program(g, core, T, topo):
 
     turn(0, pick(0))
     spread(1, D, T.psm)
+    need("v", i_rho)
+    ts(T.pmat[:, 384:512], T.rho[:], pc, None, Op.is_equal)
+    perms[D - 1] = ts(T.pmat[:, 256:384], T.rho[:], pc, 64.0, Op.is_equal, Op.mult)
     cast(0)
     for n in range(STEPS):
         a, h, b = CUT_LAST.get(n, CUT)

@@ -8,24 +8,31 @@ RW = 64
 SEL = 264
 
 SCRATCH = {}
-for _t, _names in ((BF, "xb0 128 xb1 128 xt0 128 xt1 128 oht 512 oh 512 glb 32 sel 528 rr0 1024 rr1 1024 tab0 4096 tab1 4096 "
-                        "rowq 128 rowe 128 rowa 128 rho 128 rowd 8 pmat 512 e0 128 land0 2560 land1 2560 land2 2560 land3 2560"),
-                   (F16, "amat 128 bm 32"),
-                   (F32, "wkf 4 wqf 4 ysb0 128 ysb1 128 pcol 1 pf 2 step 32 col 32"),
-                   (I32, "xi0 128 xi1 128 gl 32 wi 4 wki 4 wqi 4 pint 1 pk 2"),
-                   (U16, "offs0 64 offs1 64 lst 32")):
+for _t, _names in ((BF, "xb0 128 xb1 128 xt0 128 xt1 128 oht 512 sel 528 rr0 1024 rr1 1024 tab0 4096 tab1 4096 "
+                        "rowq 128 rowe 128 rowa 32 rho 256 pmat 768 e0 128 land0 1024 land1 2560 land2 2560 land3 2560 "
+                        "own 256 agive 32 bg 8 oh 512 nlb 4 q64 1"),
+                   (F16, "amat 32 bm 32"),
+                   (F32, "wf 4 pcol 2 pf 5 gf 1 w0 3"),
+                   (I32, "xi0 128 xi1 128 gi 4 nl 4 wi 4 pint 2 pk 5 wq 1"),
+                   (U16, "offs0 64 offs1 64 lst 32 glist 8")):
     _w = _names.split()
     for _k in range(0, len(_w), 2):
         SCRATCH[_w[_k]] = ("sbuf", [128, int(_w[_k + 1])], _t)
+SCRATCH["gall"] = ("dram", [8, 128, 4], I32)
+for _n in ("ysb0", "ysb1"):
+    SCRATCH[_n] = ("sbuf", [128, 8, 16], F32)
 for _n in ("psg0", "psg1", "psg2", "psg3", "psa0", "psa1", "psm", "psw"):
     SCRATCH[_n] = ("psum", [128, 512], F32)
 
-SEMAPHORES = ["qv", "qs", "qp", "qg", "loc", "dgive", "dwire", "dx0", "dx1", "dt0", "dt1", "dy", "arrg"]
+SEMAPHORES = ["qv", "qs", "qp", "qg", "loc", "locg", "dgive", "dgall", "dnl", "dwire", "dx0", "dx1", "dt0", "dt1", "dy", "arrg"]
 SEMAPHORES += ["arr%d" % _n for _n in range(STEPS)]
 
-CUT = (22, 32, 44)
-CUT_LAST = {15: (16, 32, 48)}
-HALF, EARLY, EVAC = 1, 1, "v"
+CUT = (26, 32, 40)
+CUT_LAST = dict([(_n, (28, 32, 40)) for _n in range(1, 15, 2)] + [(15, (16, 32, 48))])
+ORDER = "rest ps turn v0 s1 ov half cast s3 v2"
+ORDER_LAST = {15: "rest v0 s1 half s3 v2 ov"}
+WIDE = 16
+LATE = 0
 LOADS = {0: [0], 1: [1, 2], 2: [3], 3: [4], 4: [5], 5: [6], 6: [7]}
 
 
@@ -84,58 +91,69 @@ def rank_program(g, core, T, topo):
     n_eng = len([k for k in topo.engines(core, others[0]) if engines >> k & 1])
     arrive = n_eng * len(others)
 
-    def send(name, arr, lo, hi, *tokens):
-        need("g", *tokens)
+    eng = [e for e in topo.engines(core, others[0]) if engines >> e & 1]
+
+    def send(part, arr, tok, loc="loc"):
+        need("g", tok)
         ids = [DstId(rid=topo.addr(dst)[0], pnc=topo.addr(dst)[1]) for dst in others]
-        part = T[name][:, lo:hi]
         g.remote_dma_fused([RemoteDMATransfer(dst_ids=ids, dma_engine_mask=engines, remote_sem=T.sem[arr],
-                                              srcs=[part], dsts=[part] * len(others))], local_sem=T.sem["loc"])
-        count["loc"] = count.get("loc", 0) + n_eng
+                                              srcs=[part], dsts=[part] * len(others))], local_sem=T.sem[loc])
+        count[loc] = count.get(loc, 0) + n_eng
 
     t_x = {}
 
     def load_x(q, b, gb):
-        for z in range(2):
-            at = 128 * b + 64 * z
-            t_x[b] = dma(q, T["xi%d" % b][z::2, 64 * gb:64 * gb + 64], T.x[64 * gb:64 * gb + 64, at:at + 64], "dx%d" % b)
+        t_x[b] = dma(q, T["xi%d" % b][:, 64 * gb:64 * gb + 64], T.x[64 * gb:64 * gb + 64, 128 * b:128 * b + 128], "dx%d" % b)
 
-    mine = 4 * (N - 1 - rank)
-    t_give = dma("y", T.gl[:, mine:mine + 4], T.give[:, :], "dgive")
+    t_gall = dma("y", T.gall[rank], T.give[:, :], "dgall")
     load_x("s", 0, 0)
     load_x("y", 0, 1)
-    load_x("s", 1, 0)
-    load_x("y", 1, 1)
+    t_give = dma("s", T.gi[:], T.give[:, :], "dgive")
+    load_x("y", 1, 0)
+    load_x("s", 1, 1)
     t_wire = dma("s", T.wi[:], T.wires[:, :], "dwire")
     W = 8 * 4096
     t_tab = {}
-    dma("y", T.tab0[0::2, :], T.tb[:, 0:W], "dt0")
-    t_tab[0] = t_tab[1] = dma("y", T.tab0[1::2, :], T.tb[:, W:2 * W], "dt0")
 
     def load_tables(k):
         e, j = 2 + k // 4, k % 4
         t_tab[2] = t_tab[3] = dma("y", T.tab1[32 * j + e % 2:32 * j + 32:2, :], T.tb[2 * j:2 * j + 2, e * W:e * W + W], "dt1")
 
-    i_pcol = iota(T.pcol[:], [[0, 1]], 0, 1)
-    i_rowe = iota(T.rowe[:], [[8, 4], [32, 4], [1, 8]], 0, 0)
+    for k in LOADS.get(-1, ()):
+        load_tables(k)
+    dma("y", T.tab0[0::2, :], T.tb[:, 0:W], "dt0")
+    if LATE < 8:
+        t_tab[0] = t_tab[1] = dma("y", T.tab0[1:128 - 16 * LATE:2, :], T.tb[0:8 - LATE, W:2 * W], "dt0")
+
+    i_pcol = iota(T.pcol[:], [[16 * (N - 1 - rank), 2]], 0, 1)
     i_rowq = iota(T.rowq[:], [[1, 128]], 0, 0)
-    i_rowa = iota(T.rowa[:], [[0, 8], [16, 2], [1, 8]], 0, 0)
-    send("gl", "arrg", mine, mine + 4, t_give)
+    i_rowe = iota(T.rowe[:], [[8, 4], [32, 4], [1, 8]], 0, 0)
+    i_rowa = iota(T.rowa[:], [[0, 2], [16, 2], [1, 8]], 0, 0)
+    send(T.gall[rank], "arrg", t_gall, "locg")
 
     pc = T.pcol[:, 0:1]
     ident = T.pmat[:, 128:256]
     c_zero = done("v", g.vector.memset(T.sel[:], 0.0))
     need("v", i_pcol)
     c = copy("v", T.pint[:], T.pcol[:])
-    need("v", c, i_rowe)
-    ts(T.pk[:, 0:1], T.pint[:], 104, None, Op.bitwise_and)
-    c = ts(T.pk[:, 1:2], T.pint[:], 23, None, Op.bitwise_and)
-    c_e0 = ts(T.e0[:], T.rowe[:], pc, None, Op.is_equal)
-    need("v", c, i_rowq)
-    c_pf = copy("v", T.pf[:], T.pk[:])
+    need("v", c)
+    for k, bits in enumerate((104, 23, 15)):
+        ts(T.pk[:, k:k + 1], T.pint[:, 0:1], bits, None, Op.bitwise_and)
+    c = ts(T.pk[:, 3:5], T.pint[:], 112, None, Op.bitwise_and)
+    need("v", i_rowq)
     c_id = ts(ident, T.rowq[:], pc, None, Op.is_equal)
-    c_rowd = ts(T.rowd[:], T.rowq[:, 0:8], 1024.0, None, Op.mult)
+    need("v", c, i_rowe)
+    c_pf = copy("v", T.pf[:], T.pk[:])
+    c_e0 = ts(T.e0[:], T.rowe[:], pc, None, Op.is_equal)
     need("s", c_id)
     perms = {0: done("s", g.scalar.activation(T.pmat[:, 0:128], ident, Copy, scale=64.0))}
+    t_l = {}
+    hold = {}
+
+    def to_groups(out, mat, cols):
+        for k in range(4):
+            inst = mm(out[0][32 * k:32 * k + 32, out[1]:out[2]], mat, cols, True, True)
+        return done("p", inst)
 
     t_own = {}
     p_x = {}
@@ -143,8 +161,16 @@ def rank_program(g, core, T, topo):
     def codes(b):
         need("v", t_x[b])
         x1 = copy("v", T["xb%d" % b][:], T["xi%d" % b][:])
+        if b == 0:
+            need("v", t_give, c_pf)
+            c_gf = copy("v", T.gf[:], T.gi[:, 0:1])
+            for k in range(2):
+                ts(T.agive[:, 16 * k:16 * k + 16], T.rowq[:, 0:16], T.pf[:, 2:3], None, Op.is_equal)
         need("v", x1)
         x2 = done("v", g.vector.transpose(T["xt%d" % b][:], T["xb%d" % b][:]))
+        if b == 0:
+            need("v", c_gf)
+            c_bg = ts(T.bg[:], T.rowq[:, 0:128:16], T.pf[:, 4:5], T.gf[:, 0:1], Op.is_equal, Op.mult)
         need("p", x2, c_e0)
         for b0 in range(2):
             for gb in range(2):
@@ -153,68 +179,80 @@ def rank_program(g, core, T, topo):
                     inst = mm(T["psg%d" % (2 * b + b0)][64 * z:64 * z + 64, 32 * gb:32 * gb + 32],
                               T["xt%d" % b][:, 64 * gb:64 * gb + 64], T.e0[:, at:at + 32], True, True)
             p_x[2 * b + b0] = done("p", inst)
+            if b + b0 == 0:
+                need("p", c_bg)
+                hold["g"] = to_groups((T.psw, 0, 8), T.agive[:], T.bg[:])
 
     def hand_on(n, tok, q="s"):
         need(q, tok)
         at = 8 * RW * (n % 4) + RW * rank
         t_own[n] = copy(q, T["land%d" % (n // 4)][:, at:at + RW], T["psg%d" % (n % 4)][:, 0:RW])
-        send("land%d" % (n // 4), "arr%d" % n, at, at + RW, t_own[n])
+        send(T["land%d" % (n // 4)][:, at:at + RW], "arr%d" % n, t_own[n])
+
+    per = n_eng // N
+
+    def lines(c, q):
+        at, w = 256 * c, 8 // len(q)
+        for k, qq in enumerate(q):
+            need(qq, hold["x", c], hold["gl"])
+            t_own[c] = copy(qq, T.land0[:, at + 16 * w * k:at + 16 * w * (k + 1)],
+                            T.own[:, 64 * c:64 * c + 64].indirect(T.glist[:, w * k:w * (k + 1)]))
+            need("g", t_own[c])
+        parts = []
+        for k, dst in enumerate(others):
+            to = at + 128 + 16 * (N - 2 - k)
+            parts.append(RemoteDMATransfer(dst_ids=[DstId(rid=topo.addr(dst)[0], pnc=topo.addr(dst)[1])],
+                                           dma_engine_mask=sum(1 << e for e in eng[per * k:per * k + per]),
+                                           remote_sem=T.sem["arr%d" % c], srcs=[T.land0[:, at + 16 * k:at + 16 * k + 16]],
+                                           dsts=[T.land0[:, to:to + 16]]))
+        g.remote_dma_fused(parts, local_sem=T.sem["loc"])
+        count["loc"] = count.get("loc", 0) + per * len(others)
+
+    def own(c, q):
+        need(q, p_x[c])
+        hold["x", c] = copy(q, T.own[:, 64 * c:64 * c + 64], T["psg%d" % c][:, 0:64])
 
     codes(0)
     codes(1)
-    hand_on(0, p_x[0])
-    hand_on(1, p_x[1])
-    hand_on(2, p_x[2])
-    hand_on(3, p_x[3])
-    i_rho = iota(T.rho[:], [[1, 32], [32, 2], [64, 2]], 0, 0)
-
+    own(0, "v")
+    need("v", hold["g"])
+    hold["gl"] = copy("v", T.glist[:], T.psw[:, 0:8])
+    own(1, "v")
     need("v", t_wire)
-    ts(T.wki[:], T.wi[:], 15, None, Op.bitwise_and)
-    c = ts(T.wqi[:], T.wi[:], 112, None, Op.bitwise_and)
-    need("v", c)
-    ts(T.wkf[:], T.wki[:], 16.0 * rank, None, Op.add)
-    c = ts(T.wqf[:], T.wqi[:], 64.0, -8192.0 + RW, Op.mult, Op.add)
-    need("v", c, c_rowd)
-    c_oh = {}
-    c_step = {}
-
-    def hot(a, b, bank):
-        for e in range(a, b):
-            t = ts(T.oht[:, 128 * e:128 * e + 128], T.rowq[:], T.wkf[:, e:e + 1], None, Op.is_equal)
-            need("p", t, c_id)
-            inst = mm(bank[:, 128 * e:128 * e + 128], T.oht[:, 128 * e:128 * e + 128], ident, True, True)
-        need("s", done("p", inst))
-        c_oh[a] = copy("s", T.oh[:, 128 * a:128 * b], bank[:, 128 * a:128 * b])
-        for e in range(a, b):
-            c_step[a] = ts(T.step[:, 8 * e:8 * e + 8], T.rowd[:], T.wqf[:, e:e + 1], float(RW), Op.add, Op.min)
-
-    hot(0, 1, T.psa0)
-    need("v", i_rowa, c_pf)
+    c1 = ts(T.w0[:, 0:1], T.wi[:, 0:1], 16.0 * rank, 128.0, Op.is_lt, Op.mult)
+    lines(0, "vs")
+    lines(1, "vs")
+    own(2, "s")
+    i_rho = iota(T.rho[:, 0:128], [[1, 32], [32, 2], [64, 2]], 0, 0)
+    if LATE:
+        need("y", t_own[0], ("locg", n_eng))
+        t_tab[0] = t_tab[1] = dma("y", T.tab0[129 - 16 * LATE::2, :], T.tb[8 - LATE:8, W:2 * W], "dt0")
+    own(3, "v")
+    need("v", c1, i_rowa)
+    c1 = ts(T.w0[:, 1:2], T.wi[:, 0:1], -16.0 * rank, T.w0[:, 0:1], Op.add, Op.add)
     c_am = ts(T.amat[:], T.rowa[:], T.pf[:, 1:2], None, Op.is_equal)
-    hot(1, D, T.psm)
+    c2 = copy("v", T.wf[:], T.wi[:])
 
-    need("v", t_give, ("arrg", arrive))
-    c_gl = copy("v", T.glb[:], T.gl[:])
-    t_l = {}
-    hold = {}
-
-    def units(a, b, bank):
-        need("p", c_gl, c_oh[a])
-        for e in range(a, b):
-            inst = mm(bank[:, 8 * e:8 * e + 8], T.oh[:, 128 * e:128 * e + 128], T.glb[:, e:32:4], True, True)
-        hold["u", a] = done("p", inst)
+    def units():
+        need("v", t_nl)
+        hold["u"] = copy("v", T.nlb[:], T.nl[:])
 
     def columns(a, b, bank):
-        need("v", hold["u", a], c_step[a])
-        hold["c", a] = done("v", g.vector.tensor_tensor_scan(T.col[:, 8 * a:8 * b], T.step[:, 8 * a:8 * b], bank[:, 8 * a:8 * b],
-                                                             0.0, Op.add, Op.max))
+        need("p", hold["u"], hold["oh"])
+        for e in range(a, b):
+            mm(bank[:, e:e + 1], T.oh[:, 128 * e:128 * e + 128], T.q64[:], True, False)
+            inst = mm(bank[:, e:e + 1], T.oh[:, 128 * e:128 * e + 128], T.nlb[:, e:e + 1], False, True)
+        hold["c", a] = done("p", inst)
 
     def spread(a, b, bank):
         need("v", hold["c", a])
         for e in range(a, b):
-            t = ts(T.bm[:, 8 * e:8 * e + 8], T.rowe[:, 0:64:8], T.pf[:, 0:1], T.col[:, 8 * e + 7:8 * e + 8], Op.is_equal, Op.mult)
-        need("p", t, c_am)
-        hold["l", a] = done("p", mm(bank[:, 64 + 8 * a:64 + 8 * b], T.amat[:], T.bm[:, 8 * a:8 * b], True, True))
+            t = ts(T.bm[:, 8 * e:8 * e + 8], T.rowe[:, 0:64:8], T.pf[:, 0:1], bank[:, e:e + 1] if e else T.w0[:, 1:2], Op.is_equal, Op.mult)
+        hold["s"] = t
+
+    def lists(a, b, bank):
+        need("p", hold["s"], c_am)
+        hold["l", a] = to_groups((bank, 64 + 8 * a, 64 + 8 * b), T.amat[:], T.bm[:, 8 * a:8 * b])
 
     def put(a, b, bank):
         need("v", hold["l", a])
@@ -222,26 +260,39 @@ def rank_program(g, core, T, topo):
         for e in range(a, b):
             t_l[e] = t
 
-    units(0, 1, T.psw)
-    units(1, D, T.psm)
-    columns(0, 1, T.psw)
+    hold["c", 0] = c1
     spread(0, 1, T.psw)
-    columns(1, D, T.psm)
+    lists(0, 1, T.psw)
+    lines(2, "s")
+    lines(3, "s")
+    need("y", ("arrg", arrive), t_gall, t_own[3])
+    t_nl = dma("y", T.nl[:], T.gall[:, 16 * rank:16 * rank + 16, :], "dnl")
+    need("v", c2)
+    for e in range(1, D):
+        need("p", ts(T.oht[:, 128 * e:128 * e + 128], T.rowq[:], T.wf[:, e:e + 1], None, Op.is_equal), c_id)
+        inst = mm(T.psm[:, 128 * e:128 * e + 128], T.oht[:, 128 * e:128 * e + 128], ident, True, True)
+    ts(T.q64[:], T.pf[:, 3:4], RW / 16, None, Op.mult)
     put(0, 1, T.psw)
+    p_oh = done("p", inst)
+
 
     off, tok = {}, {}
 
-    def pick(n):
-        e, at = n // 4, SEL * (n % 2)
-        need("s", ("arr%d" % n, arrive), t_l[e], t_own[n], c_zero)
-        win = T["land%d" % e][:, 8 * RW * (n % 4):8 * RW * (n % 4 + 1)]
-        return copy("s", T.sel[:, at + 1:at + 257:2], win.indirect(T.lst[:, 8 * e:8 * e + 8]))
+    def pick(n, how):
+        e, at, q = n // 4, SEL * (n % 2), how[0]
+        lo, hi = (4 * int(how[1]), 4 * int(how[1]) + 4) if how[1:] else (0, 8)
+        need(q, ("arr%d" % n, arrive if e else per * len(others)), t_l[e], t_own[n], c_zero)
+        win = T["land%d" % e][:, 8 * RW * (n % 4):8 * RW * (n % 4 + 1)] if e else T.land0[:, 256 * n + 112:256 * n + 240]
+        t = copy(q, T.sel[:, at + 1 + 32 * lo:at + 1 + 32 * hi:2], win.indirect(T.lst[:, 8 * e + lo:8 * e + hi]))
+        for i in range(lo // 4, hi // 4):
+            hold["p", n, i] = t
 
-    def turn(n, t):
+    def turn(n):
         e, at = n // 4, SEL * (n % 2)
-        pk = 256 if e == D - 1 else 0
-        need("p", t, perms[D - 1 if e == D - 1 else 0])
+        pk = 512 if n >= WIDE else 256 if e == D - 1 else 0
+        need("p", perms[D - 1 if e == D - 1 else 0])
         for i in range(2):
+            need("p", hold["p", n, i])
             for z in range(2):
                 a, b = at + 128 * i + 1 - z, pk + 128 * i + 64 * z
                 inst = mm(T["psa%d" % (n % 2)][:, 0:64], T.sel[:, a:a + 128], T.pmat[:, b:b + 64], i + z == 0, i + z == 2)
@@ -259,58 +310,69 @@ def rank_program(g, core, T, topo):
 
     def take(n, lo, hi):
         e = n // 4
-        need("p", tok["v", n], tok["s", n])
+        need("p", *[tok[q, n] for q in "vs" if (q, n) in tok])
         for z in range(2):
             for u in range(8):
-                if e < D - 1:
-                    out = T["psg%d" % (n % 4)][64 * z + lo:64 * z + hi, u:64:8]
+                rows, at = T["rr%d" % (n % 2)][:, 16 * lo + 2 * u + z:16 * hi:16], 128 + 2 * u + e % 2
+                if n < WIDE:
+                    inst = mm(T["psg%d" % (n % 4)][64 * z + lo:64 * z + hi, u:64:8], rows, T.pmat[:, at:256:16], True, True)
                 else:
-                    out = T["psg%d" % (n % 4 // 2)][64 * z + lo:64 * z + hi, 8 * (n % 2) + u:128:16]
-                inst = mm(out, T["rr%d" % (n % 2)][:, 16 * lo + 2 * u + z:16 * hi:16], T.pmat[:, 128 + 2 * u + e % 2:256:16], True, True)
+                    for k in range(2):
+                        inst = mm(T["psg%d" % (n % 4)][64 * k + lo:64 * k + hi, 8 * z + u:64:16], rows, T.pmat[:, at + 16 * k:256:32], True, True)
         return done("p", inst)
 
-    def store(b, tok_p, q, queue):
+    def store(c, tok_p, q, queue):
+        b = c // 2
         need(q, tok_p)
-        t = copy(q, T["ysb%d" % b][:], T["psg%d" % b][:, 0:128])
-        for k in range(8):
+        t = copy(q, T["ysb%d" % b][:, :, 8 * (c % 2):8 * (c % 2) + 8], T["psg%d" % c][:, 0:64])
+        w = 1 if 12 + c < WIDE else 2
+        for k in range(8 // w * (c % 2)):
             need(queue[k % 2], t)
-            hold["y"] = dma(queue[k % 2], T.y[16 * k:16 * k + 16, 128 * b:128 * b + 128], T["ysb%d" % b][:, 16 * k:16 * k + 16], "dy")
+            hold["y"] = dma(queue[k % 2], T.y[16 * w * k:16 * w * (k + 1), 128 * b:128 * b + 128], T["ysb%d" % b][:, w * k:w * k + w, :], "dy")
 
-    turn(0, pick(0))
-    spread(1, D, T.psm)
-    need("v", i_rho)
-    ts(T.pmat[:, 384:512], T.rho[:], pc, None, Op.is_equal)
-    perms[D - 1] = ts(T.pmat[:, 256:384], T.rho[:], pc, 64.0, Op.is_equal, Op.mult)
+    def last_order():
+        need("v", i_rho)
+        for k in range(2):
+            if (12 < WIDE, WIDE < 16)[k]:
+                at = 256 + 256 * k
+                ts(T.pmat[:, at + 128:at + 256], T.rho[:, 128 * k:128 * k + 128], pc, None, Op.is_equal)
+                perms[D - 1] = ts(T.pmat[:, at:at + 128], T.rho[:, 128 * k:128 * k + 128], pc, 64.0, Op.is_equal, Op.mult)
+
+    extra = {(0, "v2"): units, (1, "turn"): lambda: columns(1, D, T.psm), (1, "v2"): lambda: spread(1, D, T.psm),
+             (2, "turn"): lambda: lists(1, D, T.psm), (2, "cast"): lambda: put(1, D, T.psm)}
+    pick(0, "v0")
+    pick(0, "s1")
+    turn(0)
+    last_order()
+    need("s", p_oh)
+    hold["oh"] = copy("s", T.oh[:, 128:512], T.psm[:, 128:512])
     cast(0)
     for n in range(STEPS):
-        a, h, b = CUT_LAST.get(n, CUT)
+        cut = (0,) + CUT_LAST.get(n, CUT) + (64,)
         more = n + 1 < STEPS
-        if n:
-            t = take(n - 1, hold["h"], 64)
-        hold["h"] = 32 if HALF else 0
-        if more and EARLY:
-            turn(n + 1, pick(n + 1))
-        look("v", n, 0, a)
-        look("s", n, a, h)
-        if n == 0:
-            put(1, D, T.psm)
-        if n and n + 3 < STEPS:
-            hand_on(n + 3, t, EVAC)
-        elif n == STEPS - 2:
-            store(0, t, EVAC, "yy")
-        if HALF:
-            take(n, 0, 32)
-        if more and not EARLY:
-            turn(n + 1, pick(n + 1))
-        if more and EARLY == 1:
-            cast(n + 1)
-        look("s", n, b, 64)
-        look("v", n, h, b)
-        if more and EARLY != 1:
-            cast(n + 1)
+        for op in ORDER_LAST.get(n, ORDER).split():
+            if op == "rest" and n:
+                t = take(n - 1, 32, 64)
+            elif op == "half":
+                take(n, 0, 32)
+            elif op[0] == "p" and more:
+                pick(n + 1, op[1:])
+            elif op == "turn" and more:
+                turn(n + 1)
+            elif op == "cast" and more:
+                cast(n + 1)
+            elif op[0] == "o":
+                if 0 < n < STEPS - 3:
+                    hand_on(n + 3, t, op[1])
+                elif n:
+                    store(n + 3 - STEPS, t, op[1], "yy")
+            elif op[0] in "vs":
+                look(op[0], n, cut[int(op[1])], cut[int(op[1]) + 1])
+            if (n, op) in extra:
+                extra[n, op]()
         for k in LOADS.get(n, ()):
             need("y", off[n])
             load_tables(k)
-    store(1, take(STEPS - 1, hold["h"], 64), "v", "ys")
+    store(3, take(STEPS - 1, 32, 64), "v", "ys")
     need("y", hold["y"])
-    need("g", *[(n, count[n]) for n in ("qv", "qs", "qp", "qg", "loc")])
+    need("g", *[(n, count[n]) for n in ("qv", "qs", "qp", "qg", "loc", "locg")])

from concourse.bass import DstId, RemoteDMATransfer
from concourse.mybir import dt, AluOpType, AxisListType, ActivationFunctionType

BF, F32, I32, U16, F16 = "bfloat16", "float32", "int32", "uint16", "float16"
D = 4
STEPS = 4 * D
RW = 64
SEL = 264

SCRATCH = {}
for _t, _names in ((BF, "xb0 128 xb1 128 xt0 128 xt1 128 oht 512 sel 528 rr0 1024 rr1 1024 tab0 4096 tab1 4096 "
                        "rowq 128 rowe 128 rowa 32 rho 256 pmat 768 e0 128 land0 1024 land1 2560 land2 2560 land3 2560 "
                        "own 256 agive 32 bg 8 oh 512 nlb 4 q64 1"),
                   (F16, "amat 32 bm 32"),
                   (F32, "wf 4 pcol 2 pf 5 gf 1 w0 3"),
                   (I32, "xi0 128 xi1 128 gi 4 nl 4 wi 4 pint 2 pk 5 wq 1"),
                   (U16, "offs0 64 offs1 64 lst 32 glist 8")):
    _w = _names.split()
    for _k in range(0, len(_w), 2):
        SCRATCH[_w[_k]] = ("sbuf", [128, int(_w[_k + 1])], _t)
SCRATCH["gall"] = ("dram", [8, 128, 4], I32)
for _n in ("ysb0", "ysb1"):
    SCRATCH[_n] = ("sbuf", [128, 8, 16], F32)
for _n in ("psg0", "psg1", "psg2", "psg3", "psa0", "psa1", "psm", "psw"):
    SCRATCH[_n] = ("psum", [128, 512], F32)

SEMAPHORES = ["qv", "qs", "qp", "qg", "loc", "locg", "dgive", "dgall", "dnl", "dwire", "dx0", "dx1", "dt0", "dt1", "dy", "arrg"]
SEMAPHORES += ["arr%d" % _n for _n in range(STEPS)]

CUT = (26, 32, 40)
CUT_LAST = dict([(_n, (28, 32, 40)) for _n in range(1, 15, 2)] + [(15, (16, 32, 48))])
ORDER = "rest ps turn v0 s1 ov half cast s3 v2"
ORDER_LAST = {15: "rest v0 s1 half s3 v2 ov"}
WIDE = 16
LATE = 0
LOADS = {0: [0], 1: [1, 2], 2: [3], 3: [4], 4: [5], 5: [6], 6: [7]}


def rank_program(g, core, T, topo):
    rank = T.rank_of(core)
    if rank is None:
        return
    cores = T.cores
    N = len(cores)
    Op = AluOpType
    Copy = ActivationFunctionType.Copy
    queues = {"v": g.vector, "s": g.scalar, "p": g.tensor, "g": g, "y": g.sync}
    count = {}
    seen = {}

    def need(q, *tokens):
        want = {}
        for name, val in tokens:
            want[name] = max(val, want.get(name, 0))
        for name in sorted(want):
            if seen.get((q, name), 0) < want[name]:
                queues[q].wait_ge(T.sem[name], want[name])
                seen[(q, name)] = want[name]

    def done(q, inst):
        name = "q" + q
        count[name] = count.get(name, 0) + 1
        inst.then_inc(T.sem[name], 1)
        return (name, count[name])

    def dma(q, out, in_, name):
        count[name] = count.get(name, 0) + 16
        queues[q].dma_start(out, in_).then_inc(T.sem[name], 16)
        return (name, count[name])

    def ts(out, in0, s1, s2, op0, op1=None):
        if op1 is None:
            return done("v", g.vector.tensor_scalar(out, in0, s1, s2, op0))
        return done("v", g.vector.tensor_scalar(out, in0, s1, s2, op0, op1))

    def copy(q, out, in_):
        if q == "v":
            return done("v", g.vector.tensor_copy(out, in_))
        return done("s", g.scalar.activation(out, in_, Copy))

    def iota(out, pattern, base, mult):
        return done("g", g.iota(out, pattern, base, mult, allow_small_or_imprecise_dtypes=True))

    def mm(out, lhsT, rhs, start, stop):
        return g.tensor.matmul(out, lhsT, rhs, start, stop)

    others = [cores[(rank + k) % N] for k in range(1, N)]
    engines = topo.mask(core, others[0])
    for dst in others:
        engines &= topo.mask(core, dst)
    n_eng = len([k for k in topo.engines(core, others[0]) if engines >> k & 1])
    arrive = n_eng * len(others)

    eng = [e for e in topo.engines(core, others[0]) if engines >> e & 1]

    def send(part, arr, tok, loc="loc"):
        need("g", tok)
        ids = [DstId(rid=topo.addr(dst)[0], pnc=topo.addr(dst)[1]) for dst in others]
        g.remote_dma_fused([RemoteDMATransfer(dst_ids=ids, dma_engine_mask=engines, remote_sem=T.sem[arr],
                                              srcs=[part], dsts=[part] * len(others))], local_sem=T.sem[loc])
        count[loc] = count.get(loc, 0) + n_eng

    t_x = {}

    def load_x(q, b, gb):
        t_x[b] = dma(q, T["xi%d" % b][:, 64 * gb:64 * gb + 64], T.x[64 * gb:64 * gb + 64, 128 * b:128 * b + 128], "dx%d" % b)

    t_gall = dma("y", T.gall[rank], T.give[:, :], "dgall")
    load_x("s", 0, 0)
    load_x("y", 0, 1)
    t_give = dma("s", T.gi[:], T.give[:, :], "dgive")
    load_x("y", 1, 0)
    load_x("s", 1, 1)
    t_wire = dma("s", T.wi[:], T.wires[:, :], "dwire")
    W = 8 * 4096
    t_tab = {}

    def load_tables(k):
        e, j = 2 + k // 4, k % 4
        t_tab[2] = t_tab[3] = dma("y", T.tab1[32 * j + e % 2:32 * j + 32:2, :], T.tb[2 * j:2 * j + 2, e * W:e * W + W], "dt1")

    for k in LOADS.get(-1, ()):
        load_tables(k)
    dma("y", T.tab0[0::2, :], T.tb[:, 0:W], "dt0")
    if LATE < 8:
        t_tab[0] = t_tab[1] = dma("y", T.tab0[1:128 - 16 * LATE:2, :], T.tb[0:8 - LATE, W:2 * W], "dt0")

    i_pcol = iota(T.pcol[:], [[16 * (N - 1 - rank), 2]], 0, 1)
    i_rowq = iota(T.rowq[:], [[1, 128]], 0, 0)
    i_rowe = iota(T.rowe[:], [[8, 4], [32, 4], [1, 8]], 0, 0)
    i_rowa = iota(T.rowa[:], [[0, 2], [16, 2], [1, 8]], 0, 0)
    send(T.gall[rank], "arrg", t_gall, "locg")

    pc = T.pcol[:, 0:1]
    ident = T.pmat[:, 128:256]
    c_zero = done("v", g.vector.memset(T.sel[:], 0.0))
    need("v", i_pcol)
    c = copy("v", T.pint[:], T.pcol[:])
    need("v", c)
    for k, bits in enumerate((104, 23, 15)):
        ts(T.pk[:, k:k + 1], T.pint[:, 0:1], bits, None, Op.bitwise_and)
    c = ts(T.pk[:, 3:5], T.pint[:], 112, None, Op.bitwise_and)
    need("v", i_rowq)
    c_id = ts(ident, T.rowq[:], pc, None, Op.is_equal)
    need("v", c, i_rowe)
    c_pf = copy("v", T.pf[:], T.pk[:])
    c_e0 = ts(T.e0[:], T.rowe[:], pc, None, Op.is_equal)
    need("s", c_id)
    perms = {0: done("s", g.scalar.activation(T.pmat[:, 0:128], ident, Copy, scale=64.0))}
    t_l = {}
    hold = {}

    def to_groups(out, mat, cols):
        for k in range(4):
            inst = mm(out[0][32 * k:32 * k + 32, out[1]:out[2]], mat, cols, True, True)
        return done("p", inst)

    t_own = {}
    p_x = {}

    def codes(b):
        need("v", t_x[b])
        x1 = copy("v", T["xb%d" % b][:], T["xi%d" % b][:])
        if b == 0:
            need("v", t_give, c_pf)
            c_gf = copy("v", T.gf[:], T.gi[:, 0:1])
            for k in range(2):
                ts(T.agive[:, 16 * k:16 * k + 16], T.rowq[:, 0:16], T.pf[:, 2:3], None, Op.is_equal)
        need("v", x1)
        x2 = done("v", g.vector.transpose(T["xt%d" % b][:], T["xb%d" % b][:]))
        if b == 0:
            need("v", c_gf)
            c_bg = ts(T.bg[:], T.rowq[:, 0:128:16], T.pf[:, 4:5], T.gf[:, 0:1], Op.is_equal, Op.mult)
        need("p", x2, c_e0)
        for b0 in range(2):
            for gb in range(2):
                for z in range(2):
                    at = 64 * z + 32 * b0
                    inst = mm(T["psg%d" % (2 * b + b0)][64 * z:64 * z + 64, 32 * gb:32 * gb + 32],
                              T["xt%d" % b][:, 64 * gb:64 * gb + 64], T.e0[:, at:at + 32], True, True)
            p_x[2 * b + b0] = done("p", inst)
            if b + b0 == 0:
                need("p", c_bg)
                hold["g"] = to_groups((T.psw, 0, 8), T.agive[:], T.bg[:])

    def hand_on(n, tok, q="s"):
        need(q, tok)
        at = 8 * RW * (n % 4) + RW * rank
        t_own[n] = copy(q, T["land%d" % (n // 4)][:, at:at + RW], T["psg%d" % (n % 4)][:, 0:RW])
        send(T["land%d" % (n // 4)][:, at:at + RW], "arr%d" % n, t_own[n])

    per = n_eng // N

    def lines(c, q):
        at, w = 256 * c, 8 // len(q)
        for k, qq in enumerate(q):
            need(qq, hold["x", c], hold["gl"])
            t_own[c] = copy(qq, T.land0[:, at + 16 * w * k:at + 16 * w * (k + 1)],
                            T.own[:, 64 * c:64 * c + 64].indirect(T.glist[:, w * k:w * (k + 1)]))
            need("g", t_own[c])
        parts = []
        for k, dst in enumerate(others):
            to = at + 128 + 16 * (N - 2 - k)
            parts.append(RemoteDMATransfer(dst_ids=[DstId(rid=topo.addr(dst)[0], pnc=topo.addr(dst)[1])],
                                           dma_engine_mask=sum(1 << e for e in eng[per * k:per * k + per]),
                                           remote_sem=T.sem["arr%d" % c], srcs=[T.land0[:, at + 16 * k:at + 16 * k + 16]],
                                           dsts=[T.land0[:, to:to + 16]]))
        g.remote_dma_fused(parts, local_sem=T.sem["loc"])
        count["loc"] = count.get("loc", 0) + per * len(others)

    def own(c, q):
        need(q, p_x[c])
        hold["x", c] = copy(q, T.own[:, 64 * c:64 * c + 64], T["psg%d" % c][:, 0:64])

    codes(0)
    codes(1)
    own(0, "v")
    need("v", hold["g"])
    hold["gl"] = copy("v", T.glist[:], T.psw[:, 0:8])
    own(1, "v")
    need("v", t_wire)
    c1 = ts(T.w0[:, 0:1], T.wi[:, 0:1], 16.0 * rank, 128.0, Op.is_lt, Op.mult)
    lines(0, "vs")
    lines(1, "vs")
    own(2, "s")
    i_rho = iota(T.rho[:, 0:128], [[1, 32], [32, 2], [64, 2]], 0, 0)
    if LATE:
        need("y", t_own[0], ("locg", n_eng))
        t_tab[0] = t_tab[1] = dma("y", T.tab0[129 - 16 * LATE::2, :], T.tb[8 - LATE:8, W:2 * W], "dt0")
    own(3, "v")
    need("v", c1, i_rowa)
    c1 = ts(T.w0[:, 1:2], T.wi[:, 0:1], -16.0 * rank, T.w0[:, 0:1], Op.add, Op.add)
    c_am = ts(T.amat[:], T.rowa[:], T.pf[:, 1:2], None, Op.is_equal)
    c2 = copy("v", T.wf[:], T.wi[:])

    def units():
        need("v", t_nl)
        hold["u"] = copy("v", T.nlb[:], T.nl[:])

    def columns(a, b, bank):
        need("p", hold["u"], hold["oh"])
        for e in range(a, b):
            mm(bank[:, e:e + 1], T.oh[:, 128 * e:128 * e + 128], T.q64[:], True, False)
            inst = mm(bank[:, e:e + 1], T.oh[:, 128 * e:128 * e + 128], T.nlb[:, e:e + 1], False, True)
        hold["c", a] = done("p", inst)

    def spread(a, b, bank):
        need("v", hold["c", a])
        for e in range(a, b):
            t = ts(T.bm[:, 8 * e:8 * e + 8], T.rowe[:, 0:64:8], T.pf[:, 0:1], bank[:, e:e + 1] if e else T.w0[:, 1:2], Op.is_equal, Op.mult)
        hold["s"] = t

    def lists(a, b, bank):
        need("p", hold["s"], c_am)
        hold["l", a] = to_groups((bank, 64 + 8 * a, 64 + 8 * b), T.amat[:], T.bm[:, 8 * a:8 * b])

    def put(a, b, bank):
        need("v", hold["l", a])
        t = copy("v", T.lst[:, 8 * a:8 * b], bank[:, 64 + 8 * a:64 + 8 * b])
        for e in range(a, b):
            t_l[e] = t

    hold["c", 0] = c1
    spread(0, 1, T.psw)
    lists(0, 1, T.psw)
    lines(2, "s")
    lines(3, "s")
    need("y", ("arrg", arrive), t_gall, t_own[3])
    t_nl = dma("y", T.nl[:], T.gall[:, 16 * rank:16 * rank + 16, :], "dnl")
    need("v", c2)
    for e in range(1, D):
        need("p", ts(T.oht[:, 128 * e:128 * e + 128], T.rowq[:], T.wf[:, e:e + 1], None, Op.is_equal), c_id)
        inst = mm(T.psm[:, 128 * e:128 * e + 128], T.oht[:, 128 * e:128 * e + 128], ident, True, True)
    ts(T.q64[:], T.pf[:, 3:4], RW / 16, None, Op.mult)
    put(0, 1, T.psw)
    p_oh = done("p", inst)


    off, tok = {}, {}

    def pick(n, how):
        e, at, q = n // 4, SEL * (n % 2), how[0]
        lo, hi = (4 * int(how[1]), 4 * int(how[1]) + 4) if how[1:] else (0, 8)
        need(q, ("arr%d" % n, arrive if e else per * len(others)), t_l[e], t_own[n], c_zero)
        win = T["land%d" % e][:, 8 * RW * (n % 4):8 * RW * (n % 4 + 1)] if e else T.land0[:, 256 * n + 112:256 * n + 240]
        t = copy(q, T.sel[:, at + 1 + 32 * lo:at + 1 + 32 * hi:2], win.indirect(T.lst[:, 8 * e + lo:8 * e + hi]))
        for i in range(lo // 4, hi // 4):
            hold["p", n, i] = t

    def turn(n):
        e, at = n // 4, SEL * (n % 2)
        pk = 512 if n >= WIDE else 256 if e == D - 1 else 0
        need("p", perms[D - 1 if e == D - 1 else 0])
        for i in range(2):
            need("p", hold["p", n, i])
            for z in range(2):
                a, b = at + 128 * i + 1 - z, pk + 128 * i + 64 * z
                inst = mm(T["psa%d" % (n % 2)][:, 0:64], T.sel[:, a:a + 128], T.pmat[:, b:b + 64], i + z == 0, i + z == 2)
        hold["a", n] = done("p", inst)

    def cast(n):
        need("v", hold["a", n])
        off[n] = copy("v", T["offs%d" % (n % 2)][:], T["psa%d" % (n % 2)][:, 0:64])

    def look(q, n, lo, hi):
        if lo < hi:
            need(q, t_tab[n // 4], off[n])
            win = T["tab%d" % (n // 8)][:, :].indirect(T["offs%d" % (n % 2)][:, lo:hi])
            tok[q, n] = copy(q, T["rr%d" % (n % 2)][:, 16 * lo:16 * hi], win)

    def take(n, lo, hi):
        e = n // 4
        need("p", *[tok[q, n] for q in "vs" if (q, n) in tok])
        for z in range(2):
            for u in range(8):
                rows, at = T["rr%d" % (n % 2)][:, 16 * lo + 2 * u + z:16 * hi:16], 128 + 2 * u + e % 2
                if n < WIDE:
                    inst = mm(T["psg%d" % (n % 4)][64 * z + lo:64 * z + hi, u:64:8], rows, T.pmat[:, at:256:16], True, True)
                else:
                    for k in range(2):
                        inst = mm(T["psg%d" % (n % 4)][64 * k + lo:64 * k + hi, 8 * z + u:64:16], rows, T.pmat[:, at + 16 * k:256:32], True, True)
        return done("p", inst)

    def store(c, tok_p, q, queue):
        b = c // 2
        need(q, tok_p)
        t = copy(q, T["ysb%d" % b][:, :, 8 * (c % 2):8 * (c % 2) + 8], T["psg%d" % c][:, 0:64])
        w = 1 if 12 + c < WIDE else 2
        for k in range(8 // w * (c % 2)):
            need(queue[k % 2], t)
            hold["y"] = dma(queue[k % 2], T.y[16 * w * k:16 * w * (k + 1), 128 * b:128 * b + 128], T["ysb%d" % b][:, w * k:w * k + w, :], "dy")

    def last_order():
        need("v", i_rho)
        for k in range(2):
            if (12 < WIDE, WIDE < 16)[k]:
                at = 256 + 256 * k
                ts(T.pmat[:, at + 128:at + 256], T.rho[:, 128 * k:128 * k + 128], pc, None, Op.is_equal)
                perms[D - 1] = ts(T.pmat[:, at:at + 128], T.rho[:, 128 * k:128 * k + 128], pc, 64.0, Op.is_equal, Op.mult)

    extra = {(0, "v2"): units, (1, "turn"): lambda: columns(1, D, T.psm), (1, "v2"): lambda: spread(1, D, T.psm),
             (2, "turn"): lambda: lists(1, D, T.psm), (2, "cast"): lambda: put(1, D, T.psm)}
    pick(0, "v0")
    pick(0, "s1")
    turn(0)
    last_order()
    need("s", p_oh)
    hold["oh"] = copy("s", T.oh[:, 128:512], T.psm[:, 128:512])
    cast(0)
    for n in range(STEPS):
        cut = (0,) + CUT_LAST.get(n, CUT) + (64,)
        more = n + 1 < STEPS
        for op in ORDER_LAST.get(n, ORDER).split():
            if op == "rest" and n:
                t = take(n - 1, 32, 64)
            elif op == "half":
                take(n, 0, 32)
            elif op[0] == "p" and more:
                pick(n + 1, op[1:])
            elif op == "turn" and more:
                turn(n + 1)
            elif op == "cast" and more:
                cast(n + 1)
            elif op[0] == "o":
                if 0 < n < STEPS - 3:
                    hand_on(n + 3, t, op[1])
                elif n:
                    store(n + 3 - STEPS, t, op[1], "yy")
            elif op[0] in "vs":
                look(op[0], n, cut[int(op[1])], cut[int(op[1]) + 1])
            if (n, op) in extra:
                extra[n, op]()
        for k in LOADS.get(n, ()):
            need("y", off[n])
            load_tables(k)
    store(3, take(STEPS - 1, 32, 64), "v", "ys")
    need("y", hold["y"])
    need("g", *[(n, count[n]) for n in ("qv", "qs", "qp", "qg", "loc", "locg")])
